import numpy as np
import ml_dtypes


def mxq(x, axis, fmt="e4m3"):
    dtype, down = {"e4m3": (ml_dtypes.float8_e4m3fn, 7), "e5m2": (ml_dtypes.float8_e5m2, 14)}[fmt]
    v = np.moveaxis(np.asarray(x, np.float32).astype(ml_dtypes.bfloat16).astype(np.float64), axis, -1)
    blocks = v.reshape(v.shape[:-1] + (-1, 32))
    amax = np.abs(blocks).max(-1, keepdims=True)
    byte = np.maximum(np.where(amax > 0, np.frexp(amax)[1] - 1 + 127, 0) - down, 1)
    scale = np.exp2(byte - 127.0)
    codes = (blocks / scale).astype(np.float32).astype(dtype).astype(np.float64)
    return np.moveaxis((codes * scale).reshape(v.shape), -1, axis)


WIDE = False


def mx_kscale(k):
    if not WIDE:
        return np.ones(k)
    levels = np.array([10, -10, 5, -5, 0])
    if k % 512:
        return np.exp2(np.random.permutation(np.resize(levels, k // 32))).repeat(32)
    a = np.empty((k // 512, 16))
    for p in range(k // 512):
        a[p, :8] = np.random.permutation(np.resize(levels, 8))
        for g in range(8):
            far = levels[np.abs(levels - a[p, g]) >= 10]
            a[p, g + 8] = far[np.random.randint(len(far))]
    return np.exp2(a.ravel()).repeat(32)


def f64(x):
    return np.asarray(x).astype(np.float64)


def striped(idx):
    return np.tile(np.asarray(idx).reshape(-1, 16).T, (8, 1)).astype(np.uint16)


def unstriped(offs):
    return offs[:16].T.reshape(-1).astype(np.int64)


D, T, I, Q, E = 512, 2048, 512, 128, 512


def setup_inputs():
    n = np.random.standard_normal
    idx = np.random.permutation(T)[:I]
    fd = mx_kscale(D)
    fi = mx_kscale(I)
    ti = np.ones(T)
    ti[idx] = fi
    return {
        "query": (n((D, Q)) * 0.4 / np.sqrt(D) * fd[:, None]).astype(np.float32),
        "keys": (n((D, T)) / fd[:, None]).astype(np.float32),
        "size": (np.random.uniform(0.5, 2.0, (1, I)) * fi).astype(np.float32),
        "vals": (n((E, T)) / ti).astype(np.float32),
        "offs": striped(idx),
    }


def reference(query, keys, size, vals, offs):
    idx = unstriped(offs)
    km = f64(keys)[:, idx] - np.mean(f64(keys)[:, idx], axis=1, keepdims=True)
    queryq = mxq(f64(query), 0, "e4m3")
    kmq = mxq(km, 0, "e4m3")
    a = queryq.T @ kmq
    p = np.exp(a - np.max(a, axis=1, keepdims=True))
    w = p * f64(size) / np.sum(p, axis=1, keepdims=True)
    wt = w.T
    vt = f64(vals)[:, idx].T
    wtq = mxq(wt, 0, "e4m3")
    vtq = mxq(vt, 0, "e4m3")
    o = wtq.T @ vtq
    return o

@@ -1,0 +1,135 @@
+from contextlib import ExitStack
+
+import concourse.mybir as mybir
+from concourse.masks import make_identity
+
+D, T, I, Q, E = 512, 2048, 512, 128, 512
+FLOPS = 2 * Q * I * D + 2 * Q * I * E
+
+F32 = mybir.dt.float32
+BF16 = mybir.dt.bfloat16
+U32 = mybir.dt.uint32
+U16 = mybir.dt.uint16
+U8 = mybir.dt.uint8
+FP8X4 = mybir.dt.float8_e4m3fn_x4
+ACT = mybir.ActivationFunctionType
+ALU = mybir.AluOpType
+AXIS = mybir.AxisListType
+
+P = 128
+PACK = 4
+PAIRS = 2
+VECTOR_SLOTS = 320
+
+
+def tile_attend_smoothkeys_kernel(tc, query, keys, size, vals, offs, out):
+    nc = tc.nc
+    with ExitStack() as ctx:
+        held = ctx.enter_context(tc.tile_pool(name="held", bufs=1))
+        psum = ctx.enter_context(tc.psum_pool(name="psum", bufs=1))
+        turn = ctx.enter_context(tc.psum_pool(name="turn", bufs=2))
+
+        offsets = held.tile([P, I // 16], U16, name="offsets")
+        key_planes = [held.tile([P, T], F32, name="keys%d" % t) for t in range(PACK)]
+        val_rows = [held.tile([P, T], F32, name="vals%d" % b) for b in range(E // P)]
+        query_raw = held.tile([P, PACK, Q], F32, name="query_raw")
+        size_cols = held.tile([P, PACK], F32, name="size_cols")
+
+        keys_by_plane = keys.rearrange("(p t) n -> p t n", t=PACK)
+        nc.sync.dma_start(key_planes[0][:], keys_by_plane[:, 0, :])
+        nc.sync.dma_start(offsets[:], offs)
+        for t in range(1, PACK):
+            nc.sync.dma_start(key_planes[t][:], keys_by_plane[:, t, :])
+        nc.sync.dma_start(query_raw[:], query.rearrange("(p t) q -> p t q", t=PACK))
+        nc.sync.dma_start(size_cols[:], size.rearrange("o (p t) -> (o p) t", t=PACK))
+        for b in range(E // P):
+            nc.sync.dma_start(val_rows[b][:], vals[b * P : (b + 1) * P, :])
+
+        ident = held.tile([P, P], F32, name="ident")
+        make_identity(nc, ident[:])
+
+        def quantise(name, grouped, width):
+            codes = held.tile([P, width], U32, name=name + "_codes", align_bytes=64)
+            scales = held.tile([P, width], U8, name=name + "_scales", align_bytes=64)
+            nc.vector.quantize_mx(out=codes[:].bitcast(FP8X4), scales=scales[:], in_=grouped)
+            return codes, scales
+
+        def turn_slots(name, rows):
+            words = rows[:].bitcast(F32)
+            bank = turn.tile([P, PAIRS, P], F32, name="turned")
+            for u in range(PAIRS):
+                nc.tensor.transpose(bank[:, u, :], words[:, u :: PAIRS], ident[:])
+            grouped = held.tile([P, P * PACK], BF16, name=name + "_grouped", align_bytes=64)
+            nc.scalar.copy(
+                grouped[:].bitcast(F32).rearrange("p (c u) -> p c u", u=PAIRS),
+                bank[:].rearrange("p u c -> p c u"),
+            )
+            return grouped
+
+        km = held.tile([P, I, PACK], BF16, name="km", align_bytes=64)
+        for t in range(PACK):
+            listed = held.tile([P, I], F32, name="listed_keys%d" % t)
+            scaled = held.tile([P, I], BF16, name="scaled_keys")
+            neg_mean = held.tile([P, 1], F32, name="neg_mean%d" % t)
+            nc.vector.tensor_copy(listed[:], key_planes[t][:].indirect(offsets[:]))
+            nc.scalar.activation(scaled[:], listed[:], ACT.Copy, scale=-1.0 / I, accum_out=neg_mean[:])
+            nc.vector.tensor_scalar_add(km[:, :VECTOR_SLOTS, t], listed[:, :VECTOR_SLOTS], neg_mean[:])
+            nc.scalar.activation(
+                km[:, VECTOR_SLOTS:, t], listed[:, VECTOR_SLOTS:], ACT.Identity, bias=neg_mean[:], scale=1.0
+            )
+
+        query_grouped = held.tile([P, Q, PACK], BF16, name="query_grouped", align_bytes=64)
+        nc.scalar.copy(query_grouped[:], query_raw[:].rearrange("p t q -> p q t"))
+        km_codes, km_scales = quantise("km", km[:].rearrange("p i t -> p (i t)"), I)
+        q_codes, q_scales = quantise("query", query_grouped[:].rearrange("p q t -> p (q t)"), Q)
+
+        size_bank = psum.tile([P, PACK, P], F32, name="size_bank")
+        for t in range(PACK):
+            nc.tensor.transpose(size_bank[:, t, :], size_cols[:, t : t + 1].to_broadcast([P, P]), ident[:])
+
+        def gather_vals(b):
+            listed = held.tile([P, I], BF16, name="listed_vals%d" % b, align_bytes=64)
+            nc.vector.tensor_copy(listed[:], val_rows[b][:].indirect(offsets[:]))
+            return turn_slots("vt%d" % b, listed)
+
+        def multiply(b, v_codes, v_scales):
+            acc = turn.tile([Q, P], F32, name="acc")
+            nc.tensor.matmul_mx(
+                out=acc[:], lhsT=w_codes[:].bitcast(FP8X4), lhsT_scale=w_scales[:],
+                rhs=v_codes[:].bitcast(FP8X4), rhs_scale=v_scales[:], start=True, stop=True,
+            )
+            result = held.tile([Q, P], F32, name="result%d" % b)
+            nc.scalar.copy(result[:], acc[:])
+            nc.sync.dma_start(out[:, b * P : (b + 1) * P], result[:])
+
+        scores = psum.tile([Q, I], F32, name="scores")
+        nc.tensor.matmul_mx(
+            out=scores[:], lhsT=q_codes[:].bitcast(FP8X4), lhsT_scale=q_scales[:],
+            rhs=km_codes[:].bitcast(FP8X4), rhs_scale=km_scales[:], start=True, stop=True,
+        )
+        grouped0 = gather_vals(0)
+        neg_max = held.tile([Q, 1], F32, name="neg_max")
+        nc.vector.tensor_reduce(neg_max[:], scores[:], AXIS.X, ALU.max, negate=True)
+        p = held.tile([Q, I], F32, name="p")
+        row_sum = held.tile([Q, 1], F32, name="row_sum")
+        nc.scalar.activation(p[:], scores[:], ACT.Exp, bias=neg_max[:], scale=1.0, accum_out=row_sum[:])
+        grouped1 = gather_vals(1)
+        v0 = quantise("vt0", grouped0[:], P)
+        inv_sum = held.tile([Q, 1], F32, name="inv_sum")
+        nc.vector.reciprocal(inv_sum[:], row_sum[:])
+        w = held.tile([Q, I], BF16, name="w", align_bytes=64)
+        nc.vector.scalar_tensor_tensor(
+            w[:].rearrange("q (s t) -> q s t", t=PACK), p[:].rearrange("q (s t) -> q s t", t=PACK),
+            inv_sum[:], size_bank[:].rearrange("q t s -> q s t"), ALU.mult, ALU.mult,
+        )
+        w_grouped = turn_slots("wt", w)
+        v1 = quantise("vt1", grouped1[:], P)
+        grouped2 = gather_vals(2)
+        w_codes, w_scales = quantise("wt", w_grouped[:], Q)
+        multiply(0, *v0)
+        multiply(1, *v1)
+        v2 = quantise("vt2", grouped2[:], P)
+        multiply(2, *v2)
+        grouped3 = gather_vals(3)
+        v3 = quantise("vt3", grouped3[:], P)
+        multiply(3, *v3)

@@ -19,7 +19,8 @@ AXIS = mybir.AxisListType
 P = 128
 PACK = 4
 PAIRS = 2
-VECTOR_SLOTS = 320
+BLOCKS = E // P
+VECTOR_SLOTS = 256
 
 
 def tile_attend_smoothkeys_kernel(tc, query, keys, size, vals, offs, out):
@@ -27,11 +28,11 @@ def tile_attend_smoothkeys_kernel(tc, query, keys, size, vals, offs, out):
     with ExitStack() as ctx:
         held = ctx.enter_context(tc.tile_pool(name="held", bufs=1))
         psum = ctx.enter_context(tc.psum_pool(name="psum", bufs=1))
-        turn = ctx.enter_context(tc.psum_pool(name="turn", bufs=2))
+        turn = ctx.enter_context(tc.psum_pool(name="turn", bufs=3))
 
         offsets = held.tile([P, I // 16], U16, name="offsets")
         key_planes = [held.tile([P, T], F32, name="keys%d" % t) for t in range(PACK)]
-        val_rows = [held.tile([P, T], F32, name="vals%d" % b) for b in range(E // P)]
+        val_rows = [held.tile([P, T], F32, name="vals%d" % b, tag="vals%d" % b, align_bytes=64) for b in range(BLOCKS)]
         query_raw = held.tile([P, PACK, Q], F32, name="query_raw")
         size_cols = held.tile([P, PACK], F32, name="size_cols")
 
@@ -42,94 +43,111 @@ def tile_attend_smoothkeys_kernel(tc, query, keys, size, vals, offs, out):
             nc.sync.dma_start(key_planes[t][:], keys_by_plane[:, t, :])
         nc.sync.dma_start(query_raw[:], query.rearrange("(p t) q -> p t q", t=PACK))
         nc.sync.dma_start(size_cols[:], size.rearrange("o (p t) -> (o p) t", t=PACK))
-        for b in range(E // P):
+        for b in range(BLOCKS):
             nc.sync.dma_start(val_rows[b][:], vals[b * P : (b + 1) * P, :])
 
         ident = held.tile([P, P], F32, name="ident")
         make_identity(nc, ident[:])
+        minus_one = held.tile([Q, 1], F32, name="minus_one")
+        nc.gpsimd.memset(minus_one[:], -1.0)
 
-        def quantise(name, grouped, width):
-            codes = held.tile([P, width], U32, name=name + "_codes", align_bytes=64)
+        def quantise(name, grouped, width, tag):
+            codes = held.tile([P, width], U32, name=name + "_codes", tag=tag, align_bytes=64)
             scales = held.tile([P, width], U8, name=name + "_scales", align_bytes=64)
             nc.vector.quantize_mx(out=codes[:].bitcast(FP8X4), scales=scales[:], in_=grouped)
             return codes, scales
 
-        def turn_slots(name, rows):
+        def turn_slots(rows, grouped):
             words = rows[:].bitcast(F32)
             bank = turn.tile([P, PAIRS, P], F32, name="turned")
             for u in range(PAIRS):
                 nc.tensor.transpose(bank[:, u, :], words[:, u :: PAIRS], ident[:])
-            grouped = held.tile([P, P * PACK], BF16, name=name + "_grouped", align_bytes=64)
             nc.scalar.copy(
-                grouped[:].bitcast(F32).rearrange("p (c u) -> p c u", u=PAIRS),
+                grouped.bitcast(F32).rearrange("p (c u) -> p c u", u=PAIRS),
                 bank[:].rearrange("p u c -> p c u"),
             )
-            return grouped
+
+        def gather_vals(b):
+            rows = held.tile([P, I], BF16, name="listed_vals%d" % b, align_bytes=64)
+            nc.vector.tensor_copy(rows[:], val_rows[b][:].indirect(offsets[:]))
+            return rows
 
         km = held.tile([P, I, PACK], BF16, name="km", align_bytes=64)
-        for t in range(PACK):
-            listed = held.tile([P, I], F32, name="listed_keys%d" % t)
-            scaled = held.tile([P, I], BF16, name="scaled_keys")
-            neg_mean = held.tile([P, 1], F32, name="neg_mean%d" % t)
-            nc.vector.tensor_copy(listed[:], key_planes[t][:].indirect(offsets[:]))
-            nc.scalar.activation(scaled[:], listed[:], ACT.Copy, scale=-1.0 / I, accum_out=neg_mean[:])
-            nc.vector.tensor_scalar_add(km[:, :VECTOR_SLOTS, t], listed[:, :VECTOR_SLOTS], neg_mean[:])
-            nc.scalar.activation(
-                km[:, VECTOR_SLOTS:, t], listed[:, VECTOR_SLOTS:], ACT.Identity, bias=neg_mean[:], scale=1.0
-            )
-
         query_grouped = held.tile([P, Q, PACK], BF16, name="query_grouped", align_bytes=64)
-        nc.scalar.copy(query_grouped[:], query_raw[:].rearrange("p t q -> p q t"))
-        km_codes, km_scales = quantise("km", km[:].rearrange("p i t -> p (i t)"), I)
-        q_codes, q_scales = quantise("query", query_grouped[:].rearrange("p q t -> p (q t)"), Q)
+        listed = held.tile([P, PACK, I], F32, name="listed_keys")
+        neg_mean = held.tile([P, PACK], F32, name="neg_mean")
+        for t in range(PACK):
+            scaled = held.tile([P, I], BF16, name="scaled_keys")
+            nc.vector.tensor_copy(listed[:, t, :], key_planes[t][:].indirect(offsets[:]))
+            nc.scalar.activation(scaled[:], listed[:, t, :], ACT.Copy, scale=-1.0 / I, accum_out=neg_mean[:, t : t + 1])
+            split = VECTOR_SLOTS if t >= 2 else 0
+            nc.scalar.activation(
+                km[:, split:, t], listed[:, t, split:], ACT.Identity, bias=neg_mean[:, t : t + 1], scale=1.0
+            )
+        nc.vector.tensor_copy(query_grouped[:], query_raw[:].rearrange("p t q -> p q t"))
+        q_codes, q_scales = quantise("query", query_grouped[:].rearrange("p q t -> p (q t)"), Q, "query_codes")
+        nc.vector.tensor_tensor(
+            km[:, :VECTOR_SLOTS, 2:],
+            listed[:, 2:, :VECTOR_SLOTS].rearrange("p t i -> p i t"),
+            neg_mean[:, 2:].unsqueeze(1).to_broadcast([P, VECTOR_SLOTS, 2]),
+            ALU.add,
+        )
+        km_codes, km_scales = quantise("km", km[:].rearrange("p i t -> p (i t)"), I, "km_codes")
 
         size_bank = psum.tile([P, PACK, P], F32, name="size_bank")
         for t in range(PACK):
             nc.tensor.transpose(size_bank[:, t, :], size_cols[:, t : t + 1].to_broadcast([P, P]), ident[:])
-
-        def gather_vals(b):
-            listed = held.tile([P, I], BF16, name="listed_vals%d" % b, align_bytes=64)
-            nc.vector.tensor_copy(listed[:], val_rows[b][:].indirect(offsets[:]))
-            return turn_slots("vt%d" % b, listed)
-
-        def multiply(b, v_codes, v_scales):
-            acc = turn.tile([Q, P], F32, name="acc")
-            nc.tensor.matmul_mx(
-                out=acc[:], lhsT=w_codes[:].bitcast(FP8X4), lhsT_scale=w_scales[:],
-                rhs=v_codes[:].bitcast(FP8X4), rhs_scale=v_scales[:], start=True, stop=True,
-            )
-            result = held.tile([Q, P], F32, name="result%d" % b)
-            nc.scalar.copy(result[:], acc[:])
-            nc.sync.dma_start(out[:, b * P : (b + 1) * P], result[:])
 
         scores = psum.tile([Q, I], F32, name="scores")
         nc.tensor.matmul_mx(
             out=scores[:], lhsT=q_codes[:].bitcast(FP8X4), lhsT_scale=q_scales[:],
             rhs=km_codes[:].bitcast(FP8X4), rhs_scale=km_scales[:], start=True, stop=True,
         )
-        grouped0 = gather_vals(0)
-        neg_max = held.tile([Q, 1], F32, name="neg_max")
+        listed0 = gather_vals(0)
+        neg_max = held.tile([Q, 1], F32, name="neg_max", tag="vals0", align_bytes=64)
         nc.vector.tensor_reduce(neg_max[:], scores[:], AXIS.X, ALU.max, negate=True)
         p = held.tile([Q, I], F32, name="p")
         row_sum = held.tile([Q, 1], F32, name="row_sum")
         nc.scalar.activation(p[:], scores[:], ACT.Exp, bias=neg_max[:], scale=1.0, accum_out=row_sum[:])
-        grouped1 = gather_vals(1)
-        v0 = quantise("vt0", grouped0[:], P)
+        early = held.tile([P, BLOCKS, P * PACK], BF16, name="early", tag="vals0", align_bytes=64)
+        turn_slots(listed0, early[:, 0, :])
+        turn_slots(gather_vals(1), early[:, 1, :])
         inv_sum = held.tile([Q, 1], F32, name="inv_sum")
-        nc.vector.reciprocal(inv_sum[:], row_sum[:])
-        w = held.tile([Q, I], BF16, name="w", align_bytes=64)
+        nc.gpsimd.tensor_tensor(inv_sum[:], row_sum[:], minus_one[:], ALU.pow)
+        listed2 = gather_vals(2)
+        w = held.tile([Q, I], BF16, name="w", tag="vals2", align_bytes=64)
         nc.vector.scalar_tensor_tensor(
             w[:].rearrange("q (s t) -> q s t", t=PACK), p[:].rearrange("q (s t) -> q s t", t=PACK),
             inv_sum[:], size_bank[:].rearrange("q t s -> q s t"), ALU.mult, ALU.mult,
         )
-        w_grouped = turn_slots("wt", w)
-        v1 = quantise("vt1", grouped1[:], P)
-        grouped2 = gather_vals(2)
-        w_codes, w_scales = quantise("wt", w_grouped[:], Q)
-        multiply(0, *v0)
-        multiply(1, *v1)
-        v2 = quantise("vt2", grouped2[:], P)
-        multiply(2, *v2)
-        grouped3 = gather_vals(3)
-        v3 = quantise("vt3", grouped3[:], P)
-        multiply(3, *v3)
+        turn_slots(listed2, early[:, 2, :])
+        turn_slots(w, early[:, 3, :])
+        late = held.tile([P, P * PACK], BF16, name="late", align_bytes=64)
+        turn_slots(gather_vals(3), late[:])
+        early_codes = held.tile([P, BLOCKS * P], U32, name="early_codes", tag="vals3", align_bytes=64)
+        early_scales = held.tile([P, BLOCKS * P], U8, name="early_scales", align_bytes=64)
+        for h in range(2):
+            cols = slice(2 * h * P, 2 * (h + 1) * P)
+            nc.vector.quantize_mx(
+                out=early_codes[:, cols].bitcast(FP8X4), scales=early_scales[:, cols],
+                in_=early[:, 2 * h : 2 * h + 2, :].rearrange("p b c -> p (b c)"),
+            )
+        late_codes, late_scales = quantise("late", late[:], P, "late_codes")
+
+        def multiply(acc, codes, scales):
+            nc.tensor.matmul_mx(
+                out=acc, lhsT=early_codes[:, 3 * P :].bitcast(FP8X4), lhsT_scale=early_scales[:, 3 * P :],
+                rhs=codes.bitcast(FP8X4), rhs_scale=scales, start=True, stop=True,
+            )
+
+        early_result = held.tile([Q, 3 * P], F32, name="early_result")
+        for name, cols in (("pair_acc", slice(0, 2 * P)), ("third_acc", slice(2 * P, 3 * P))):
+            acc = psum.tile([Q, cols.stop - cols.start], F32, name=name)
+            multiply(acc[:], early_codes[:, cols], early_scales[:, cols])
+            nc.scalar.copy(early_result[:, cols], acc[:])
+        nc.sync.dma_start(out[:, : 3 * P], early_result[:])
+        late_acc = psum.tile([Q, P], F32, name="late_acc")
+        multiply(late_acc[:], late_codes[:], late_scales[:])
+        late_result = held.tile([Q, P], F32, name="late_result")
+        nc.vector.tensor_copy(late_result[:], late_acc[:])
+        nc.sync.dma_start(out[:, 3 * P :], late_result[:])

@@ -140,12 +140,12 @@ def tile_attend_smoothkeys_kernel(tc, query, keys, size, vals, offs, out):
                 rhs=codes.bitcast(FP8X4), rhs_scale=scales, start=True, stop=True,
             )
 
-        early_result = held.tile([Q, 3 * P], F32, name="early_result")
-        for name, cols in (("pair_acc", slice(0, 2 * P)), ("third_acc", slice(2 * P, 3 * P))):
-            acc = psum.tile([Q, cols.stop - cols.start], F32, name=name)
+        for name, cols in (("pair", slice(0, 2 * P)), ("third", slice(2 * P, 3 * P))):
+            acc = psum.tile([Q, cols.stop - cols.start], F32, name=name + "_acc")
             multiply(acc[:], early_codes[:, cols], early_scales[:, cols])
-            nc.scalar.copy(early_result[:, cols], acc[:])
-        nc.sync.dma_start(out[:, : 3 * P], early_result[:])
+            result = held.tile([Q, cols.stop - cols.start], F32, name=name + "_result")
+            nc.scalar.copy(result[:], acc[:])
+            nc.sync.dma_start(out[:, cols], result[:])
         late_acc = psum.tile([Q, P], F32, name="late_acc")
         multiply(late_acc[:], late_codes[:], late_scales[:])
         late_result = held.tile([Q, P], F32, name="late_result")

@@ -20,6 +20,7 @@ P = 128
 PACK = 4
 PAIRS = 2
 BLOCKS = E // P
+HALF = I // 2
 VECTOR_SLOTS = 256
 
 
@@ -76,14 +77,34 @@ def tile_attend_smoothkeys_kernel(tc, query, keys, size, vals, offs, out):
         query_grouped = held.tile([P, Q, PACK], BF16, name="query_grouped", align_bytes=64)
         listed = held.tile([P, PACK, I], F32, name="listed_keys")
         neg_mean = held.tile([P, PACK], F32, name="neg_mean")
-        for t in range(PACK):
-            scaled = held.tile([P, I], BF16, name="scaled_keys")
+        part_mean = held.tile([P, 1], F32, name="part_mean")
+        scaled = held.tile([P, I], BF16, name="scaled_keys")
+        last = PACK - 1
+        for t in range(last):
             nc.vector.tensor_copy(listed[:, t, :], key_planes[t][:].indirect(offsets[:]))
-            nc.scalar.activation(scaled[:], listed[:, t, :], ACT.Copy, scale=-1.0 / I, accum_out=neg_mean[:, t : t + 1])
+            nc.vector.tensor_scalar(
+                scaled[:], listed[:, t, :], -1.0 / I, None, ALU.mult, ALU.add, accum_out=neg_mean[:, t : t + 1]
+            )
             split = VECTOR_SLOTS if t >= 2 else 0
             nc.scalar.activation(
                 km[:, split:, t], listed[:, t, split:], ACT.Identity, bias=neg_mean[:, t : t + 1], scale=1.0
             )
+        for h in range(2):
+            nc.vector.tensor_copy(
+                listed[:, last, h * HALF : (h + 1) * HALF],
+                key_planes[last][:].indirect(offsets[:, h * HALF // 16 : (h + 1) * HALF // 16]),
+            )
+        scaled_last = held.tile([P, I], BF16, name="scaled_last")
+        nc.scalar.activation(
+            scaled_last[:, :HALF], listed[:, last, :HALF], ACT.Copy, scale=-1.0 / (I * HALF), accum_out=part_mean[:]
+        )
+        nc.scalar.activation(
+            scaled_last[:, HALF:], listed[:, last, HALF:], ACT.Identity, bias=part_mean[:], scale=-1.0 / I,
+            accum_out=neg_mean[:, last:],
+        )
+        nc.scalar.activation(
+            km[:, VECTOR_SLOTS:, last], listed[:, last, VECTOR_SLOTS:], ACT.Identity, bias=neg_mean[:, last:], scale=1.0
+        )
         nc.vector.tensor_copy(query_grouped[:], query_raw[:].rearrange("p t q -> p q t"))
         q_codes, q_scales = quantise("query", query_grouped[:].rearrange("p q t -> p (q t)"), Q, "query_codes")
         nc.vector.tensor_tensor(
@@ -92,11 +113,13 @@ def tile_attend_smoothkeys_kernel(tc, query, keys, size, vals, offs, out):
             neg_mean[:, 2:].unsqueeze(1).to_broadcast([P, VECTOR_SLOTS, 2]),
             ALU.add,
         )
-        km_codes, km_scales = quantise("km", km[:].rearrange("p i t -> p (i t)"), I, "km_codes")
-
-        size_bank = psum.tile([P, PACK, P], F32, name="size_bank")
-        for t in range(PACK):
-            nc.tensor.transpose(size_bank[:, t, :], size_cols[:, t : t + 1].to_broadcast([P, P]), ident[:])
+        km_codes = held.tile([P, I], U32, name="km_codes", align_bytes=64)
+        km_scales = held.tile([P, I], U8, name="km_scales", align_bytes=64)
+        for cols in (slice(VECTOR_SLOTS, I), slice(0, VECTOR_SLOTS)):
+            nc.vector.quantize_mx(
+                out=km_codes[:, cols].bitcast(FP8X4), scales=km_scales[:, cols],
+                in_=km[:, cols, :].rearrange("p i t -> p (i t)"),
+            )
 
         scores = psum.tile([Q, I], F32, name="scores")
         nc.tensor.matmul_mx(
@@ -114,6 +137,10 @@ def tile_attend_smoothkeys_kernel(tc, query, keys, size, vals, offs, out):
         turn_slots(gather_vals(1), early[:, 1, :])
         inv_sum = held.tile([Q, 1], F32, name="inv_sum")
         nc.gpsimd.tensor_tensor(inv_sum[:], row_sum[:], minus_one[:], ALU.pow)
+        size_bank = psum.tile([P, PACK, P], F32, name="size_bank")
+        for t in range(PACK):
+            nc.tensor.transpose(size_bank[:, t, :], size_cols[:, t : t + 1].to_broadcast([P, P]), ident[:])
+
         listed2 = gather_vals(2)
         w = held.tile([Q, I], BF16, name="w", tag="vals2", align_bytes=64)
         nc.vector.scalar_tensor_tensor(
@@ -132,17 +159,22 @@ def tile_attend_smoothkeys_kernel(tc, query, keys, size, vals, offs, out):
                 out=early_codes[:, cols].bitcast(FP8X4), scales=early_scales[:, cols],
                 in_=early[:, 2 * h : 2 * h + 2, :].rearrange("p b c -> p (b c)"),
             )
+        pair_codes, pair_scales = early_codes[:, : 2 * P], early_scales[:, : 2 * P]
+        rest_codes, rest_scales = early_codes[:, 2 * P :], early_scales[:, 2 * P :]
         late_codes, late_scales = quantise("late", late[:], P, "late_codes")
 
         def multiply(acc, codes, scales):
             nc.tensor.matmul_mx(
-                out=acc, lhsT=early_codes[:, 3 * P :].bitcast(FP8X4), lhsT_scale=early_scales[:, 3 * P :],
+                out=acc, lhsT=rest_codes[:, P:].bitcast(FP8X4), lhsT_scale=rest_scales[:, P:],
                 rhs=codes.bitcast(FP8X4), rhs_scale=scales, start=True, stop=True,
             )
 
-        for name, cols in (("pair", slice(0, 2 * P)), ("third", slice(2 * P, 3 * P))):
+        for name, cols, codes, scales in (
+            ("pair", slice(0, 2 * P), pair_codes, pair_scales),
+            ("third", slice(2 * P, 3 * P), rest_codes[:, :P], rest_scales[:, :P]),
+        ):
             acc = psum.tile([Q, cols.stop - cols.start], F32, name=name + "_acc")
-            multiply(acc[:], early_codes[:, cols], early_scales[:, cols])
+            multiply(acc[:], codes, scales)
             result = held.tile([Q, cols.stop - cols.start], F32, name=name + "_result")
             nc.scalar.copy(result[:], acc[:])
             nc.sync.dma_start(out[:, cols], result[:])

@@ -122,33 +122,37 @@ def tile_attend_smoothkeys_kernel(tc, query, keys, size, vals, offs, out):
             )
 
         scores = psum.tile([Q, I], F32, name="scores")
-        nc.tensor.matmul_mx(
-            out=scores[:], lhsT=q_codes[:].bitcast(FP8X4), lhsT_scale=q_scales[:],
-            rhs=km_codes[:].bitcast(FP8X4), rhs_scale=km_scales[:], start=True, stop=True,
-        )
-        listed0 = gather_vals(0)
-        neg_max = held.tile([Q, 1], F32, name="neg_max", tag="vals0", align_bytes=64)
+        for cols in (slice(VECTOR_SLOTS, I), slice(0, VECTOR_SLOTS)):
+            nc.tensor.matmul_mx(
+                out=scores[:, cols], lhsT=q_codes[:].bitcast(FP8X4), lhsT_scale=q_scales[:],
+                rhs=km_codes[:, cols].bitcast(FP8X4), rhs_scale=km_scales[:, cols], start=True, stop=True,
+            )
+        first_pool = held.tile([P, T], BF16, name="first_pool", align_bytes=64)
+        nc.scalar.activation(first_pool[:], val_rows[0][:], ACT.Copy)
+        neg_max = held.tile([Q, 1], F32, name="neg_max", tag="neg_max", align_bytes=64)
         nc.vector.tensor_reduce(neg_max[:], scores[:], AXIS.X, ALU.max, negate=True)
-        p = held.tile([Q, I], F32, name="p")
+        p = held.tile([Q, I], F32, name="p", tag="vals0", align_bytes=64)
         row_sum = held.tile([Q, 1], F32, name="row_sum")
         nc.scalar.activation(p[:], scores[:], ACT.Exp, bias=neg_max[:], scale=1.0, accum_out=row_sum[:])
-        early = held.tile([P, BLOCKS, P * PACK], BF16, name="early", tag="vals0", align_bytes=64)
-        turn_slots(listed0, early[:, 0, :])
-        turn_slots(gather_vals(1), early[:, 1, :])
+        listed0 = held.tile([P, I], BF16, name="listed_vals0", tag="neg_max", align_bytes=64)
+        nc.scalar.activation(listed0[:], first_pool[:].indirect(offsets[:]), ACT.Copy)
+        early = held.tile([P, BLOCKS, P * PACK], BF16, name="early", align_bytes=64)
+        listed1 = gather_vals(1)
         inv_sum = held.tile([Q, 1], F32, name="inv_sum")
         nc.gpsimd.tensor_tensor(inv_sum[:], row_sum[:], minus_one[:], ALU.pow)
         size_bank = psum.tile([P, PACK, P], F32, name="size_bank")
         for t in range(PACK):
             nc.tensor.transpose(size_bank[:, t, :], size_cols[:, t : t + 1].to_broadcast([P, P]), ident[:])
 
-        listed2 = gather_vals(2)
-        w = held.tile([Q, I], BF16, name="w", tag="vals2", align_bytes=64)
+        w = held.tile([Q, I], BF16, name="w", tag="vals1", align_bytes=64)
         nc.vector.scalar_tensor_tensor(
             w[:].rearrange("q (s t) -> q s t", t=PACK), p[:].rearrange("q (s t) -> q s t", t=PACK),
             inv_sum[:], size_bank[:].rearrange("q t s -> q s t"), ALU.mult, ALU.mult,
         )
-        turn_slots(listed2, early[:, 2, :])
+        turn_slots(listed1, early[:, 1, :])
+        turn_slots(listed0, early[:, 0, :])
         turn_slots(w, early[:, 3, :])
+        turn_slots(gather_vals(2), early[:, 2, :])
         late = held.tile([P, P * PACK], BF16, name="late", align_bytes=64)
         turn_slots(gather_vals(3), late[:])
         early_codes = held.tile([P, BLOCKS * P], U32, name="early_codes", tag="vals3", align_bytes=64)

@@ -44,7 +44,7 @@ def tile_attend_smoothkeys_kernel(tc, query, keys, size, vals, offs, out):
             nc.sync.dma_start(key_planes[t][:], keys_by_plane[:, t, :])
         nc.sync.dma_start(query_raw[:], query.rearrange("(p t) q -> p t q", t=PACK))
         nc.sync.dma_start(size_cols[:], size.rearrange("o (p t) -> (o p) t", t=PACK))
-        for b in range(BLOCKS):
+        for b in (1, 0, 2, 3):
             nc.sync.dma_start(val_rows[b][:], vals[b * P : (b + 1) * P, :])
 
         ident = held.tile([P, P], F32, name="ident")
@@ -128,62 +128,65 @@ def tile_attend_smoothkeys_kernel(tc, query, keys, size, vals, offs, out):
                 rhs=km_codes[:, cols].bitcast(FP8X4), rhs_scale=km_scales[:, cols], start=True, stop=True,
             )
         first_pool = held.tile([P, T], BF16, name="first_pool", align_bytes=64)
-        nc.scalar.activation(first_pool[:], val_rows[0][:], ACT.Copy)
+        nc.scalar.activation(first_pool[:], val_rows[1][:], ACT.Copy)
         neg_max = held.tile([Q, 1], F32, name="neg_max", tag="neg_max", align_bytes=64)
         nc.vector.tensor_reduce(neg_max[:], scores[:], AXIS.X, ALU.max, negate=True)
-        p = held.tile([Q, I], F32, name="p", tag="vals0", align_bytes=64)
+        p = held.tile([Q, I], F32, name="p", tag="vals1", align_bytes=64)
         row_sum = held.tile([Q, 1], F32, name="row_sum")
         nc.scalar.activation(p[:], scores[:], ACT.Exp, bias=neg_max[:], scale=1.0, accum_out=row_sum[:])
-        listed0 = held.tile([P, I], BF16, name="listed_vals0", tag="neg_max", align_bytes=64)
-        nc.scalar.activation(listed0[:], first_pool[:].indirect(offsets[:]), ACT.Copy)
-        early = held.tile([P, BLOCKS, P * PACK], BF16, name="early", align_bytes=64)
-        listed1 = gather_vals(1)
+        listed1 = held.tile([P, I], BF16, name="listed_vals1", tag="neg_max", align_bytes=64)
+        nc.scalar.activation(listed1[:], first_pool[:].indirect(offsets[:]), ACT.Copy)
+        lead = held.tile([P, 2, P * PACK], BF16, name="lead", align_bytes=64)
+        pair = held.tile([P, 2, P * PACK], BF16, name="pair", align_bytes=64)
+        listed0 = gather_vals(0)
         inv_sum = held.tile([Q, 1], F32, name="inv_sum")
         nc.gpsimd.tensor_tensor(inv_sum[:], row_sum[:], minus_one[:], ALU.pow)
         size_bank = psum.tile([P, PACK, P], F32, name="size_bank")
         for t in range(PACK):
             nc.tensor.transpose(size_bank[:, t, :], size_cols[:, t : t + 1].to_broadcast([P, P]), ident[:])
 
-        w = held.tile([Q, I], BF16, name="w", tag="vals1", align_bytes=64)
+        w = held.tile([Q, I], BF16, name="w", tag="vals0", align_bytes=64)
         nc.vector.scalar_tensor_tensor(
             w[:].rearrange("q (s t) -> q s t", t=PACK), p[:].rearrange("q (s t) -> q s t", t=PACK),
             inv_sum[:], size_bank[:].rearrange("q t s -> q s t"), ALU.mult, ALU.mult,
         )
-        turn_slots(listed1, early[:, 1, :])
-        turn_slots(listed0, early[:, 0, :])
-        turn_slots(w, early[:, 3, :])
-        turn_slots(gather_vals(2), early[:, 2, :])
-        late = held.tile([P, P * PACK], BF16, name="late", align_bytes=64)
-        turn_slots(gather_vals(3), late[:])
-        early_codes = held.tile([P, BLOCKS * P], U32, name="early_codes", tag="vals3", align_bytes=64)
-        early_scales = held.tile([P, BLOCKS * P], U8, name="early_scales", align_bytes=64)
+        turn_slots(listed0, lead[:, 0, :])
+        turn_slots(w, lead[:, 1, :])
+        turn_slots(listed1, pair[:, 0, :])
+        turn_slots(gather_vals(2), pair[:, 1, :])
+        lead_codes, lead_scales = quantise("lead", lead[:].rearrange("p b c -> p (b c)"), 2 * P, "vals2")
+        last_words = gather_vals(3)[:].bitcast(F32)
+        pair_codes, pair_scales = quantise("pair", pair[:].rearrange("p b c -> p (b c)"), 2 * P, "vals3")
+        last_bank = turn.tile([P, PAIRS, P], F32, name="turned")
+        for u in range(PAIRS):
+            nc.tensor.transpose(last_bank[:, u, :], last_words[:, u :: PAIRS], ident[:])
+        last_parts = []
         for h in range(2):
-            cols = slice(2 * h * P, 2 * (h + 1) * P)
-            nc.vector.quantize_mx(
-                out=early_codes[:, cols].bitcast(FP8X4), scales=early_scales[:, cols],
-                in_=early[:, 2 * h : 2 * h + 2, :].rearrange("p b c -> p (b c)"),
+            part = held.tile([P, P * PACK // 2], BF16, name="last%d" % h, align_bytes=64)
+            nc.scalar.copy(
+                part[:].bitcast(F32).rearrange("p (c u) -> p c u", u=PAIRS),
+                last_bank[:, :, h * P // 2 : (h + 1) * P // 2].rearrange("p u c -> p c u"),
             )
-        pair_codes, pair_scales = early_codes[:, : 2 * P], early_scales[:, : 2 * P]
-        rest_codes, rest_scales = early_codes[:, 2 * P :], early_scales[:, 2 * P :]
-        late_codes, late_scales = quantise("late", late[:], P, "late_codes")
+            last_parts.append(quantise("last%d" % h, part[:], P // 2, "last_codes%d" % h))
 
         def multiply(acc, codes, scales):
             nc.tensor.matmul_mx(
-                out=acc, lhsT=rest_codes[:, P:].bitcast(FP8X4), lhsT_scale=rest_scales[:, P:],
+                out=acc, lhsT=lead_codes[:, P:].bitcast(FP8X4), lhsT_scale=lead_scales[:, P:],
                 rhs=codes.bitcast(FP8X4), rhs_scale=scales, start=True, stop=True,
             )
 
         for name, cols, codes, scales in (
-            ("pair", slice(0, 2 * P), pair_codes, pair_scales),
-            ("third", slice(2 * P, 3 * P), rest_codes[:, :P], rest_scales[:, :P]),
+            ("lead", slice(0, P), lead_codes[:, :P], lead_scales[:, :P]),
+            ("pair", slice(P, 3 * P), pair_codes[:], pair_scales[:]),
         ):
             acc = psum.tile([Q, cols.stop - cols.start], F32, name=name + "_acc")
             multiply(acc[:], codes, scales)
             result = held.tile([Q, cols.stop - cols.start], F32, name=name + "_result")
             nc.scalar.copy(result[:], acc[:])
             nc.sync.dma_start(out[:, cols], result[:])
-        late_acc = psum.tile([Q, P], F32, name="late_acc")
-        multiply(late_acc[:], late_codes[:], late_scales[:])
-        late_result = held.tile([Q, P], F32, name="late_result")
-        nc.vector.tensor_copy(late_result[:], late_acc[:])
-        nc.sync.dma_start(out[:, 3 * P :], late_result[:])
+        last_result = held.tile([Q, P], F32, name="last_result")
+        for h, (codes, scales) in enumerate(last_parts):
+            acc = turn.tile([Q, P // 2], F32, name="turned")
+            multiply(acc[:], codes[:], scales[:])
+            nc.vector.tensor_copy(last_result[:, h * P // 2 : (h + 1) * P // 2], acc[:])
+        nc.sync.dma_start(out[:, 3 * P :], last_result[:])

@@ -154,9 +154,13 @@ def tile_attend_smoothkeys_kernel(tc, query, keys, size, vals, offs, out):
         turn_slots(w, lead[:, 1, :])
         turn_slots(listed1, pair[:, 0, :])
         turn_slots(gather_vals(2), pair[:, 1, :])
-        lead_codes, lead_scales = quantise("lead", lead[:].rearrange("p b c -> p (b c)"), 2 * P, "vals2")
         last_words = gather_vals(3)[:].bitcast(F32)
-        pair_codes, pair_scales = quantise("pair", pair[:].rearrange("p b c -> p (b c)"), 2 * P, "vals3")
+        early_codes = held.tile([P, BLOCKS * P], U32, name="early_codes", tag="vals3", align_bytes=64)
+        early_scales = held.tile([P, BLOCKS * P], U8, name="early_scales", align_bytes=64)
+        lead_codes, lead_scales = early_codes[:, : 2 * P], early_scales[:, : 2 * P]
+        pair_codes, pair_scales = early_codes[:, 2 * P :], early_scales[:, 2 * P :]
+        for codes, scales, grouped in ((lead_codes, lead_scales, lead), (pair_codes, pair_scales, pair)):
+            nc.vector.quantize_mx(out=codes.bitcast(FP8X4), scales=scales, in_=grouped[:].rearrange("p b c -> p (b c)"))
         last_bank = turn.tile([P, PAIRS, P], F32, name="turned")
         for u in range(PAIRS):
             nc.tensor.transpose(last_bank[:, u, :], last_words[:, u :: PAIRS], ident[:])
@@ -177,7 +181,7 @@ def tile_attend_smoothkeys_kernel(tc, query, keys, size, vals, offs, out):
 
         for name, cols, codes, scales in (
             ("lead", slice(0, P), lead_codes[:, :P], lead_scales[:, :P]),
-            ("pair", slice(P, 3 * P), pair_codes[:], pair_scales[:]),
+            ("pair", slice(P, 3 * P), pair_codes, pair_scales),
         ):
             acc = psum.tile([Q, cols.stop - cols.start], F32, name=name + "_acc")
             multiply(acc[:], codes, scales)

@@ -154,7 +154,8 @@ def tile_attend_smoothkeys_kernel(tc, query, keys, size, vals, offs, out):
         turn_slots(w, lead[:, 1, :])
         turn_slots(listed1, pair[:, 0, :])
         turn_slots(gather_vals(2), pair[:, 1, :])
-        last_words = gather_vals(3)[:].bitcast(F32)
+        last_rows = held.tile([P, PAIRS, P, 2], BF16, name="last_rows", align_bytes=64)
+        nc.vector.tensor_copy(last_rows[:].rearrange("p u s e -> p s u e"), val_rows[3][:].indirect(offsets[:]))
         early_codes = held.tile([P, BLOCKS * P], U32, name="early_codes", tag="vals3", align_bytes=64)
         early_scales = held.tile([P, BLOCKS * P], U8, name="early_scales", align_bytes=64)
         lead_codes, lead_scales = early_codes[:, : 2 * P], early_scales[:, : 2 * P]
@@ -163,7 +164,7 @@ def tile_attend_smoothkeys_kernel(tc, query, keys, size, vals, offs, out):
             nc.vector.quantize_mx(out=codes.bitcast(FP8X4), scales=scales, in_=grouped[:].rearrange("p b c -> p (b c)"))
         last_bank = turn.tile([P, PAIRS, P], F32, name="turned")
         for u in range(PAIRS):
-            nc.tensor.transpose(last_bank[:, u, :], last_words[:, u :: PAIRS], ident[:])
+            nc.tensor.transpose(last_bank[:, u, :], last_rows[:, u, :, :].rearrange("p s e -> p (s e)").bitcast(F32), ident[:])
         last_parts = []
         for h in range(2):
             part = held.tile([P, P * PACK // 2], BF16, name="last%d" % h, align_bytes=64)

@@ -34,8 +34,9 @@ def tile_attend_smoothkeys_kernel(tc, query, keys, size, vals, offs, out):
         offsets = held.tile([P, I // 16], U16, name="offsets")
         key_planes = [held.tile([P, T], F32, name="keys%d" % t) for t in range(PACK)]
         val_rows = [held.tile([P, T], F32, name="vals%d" % b, tag="vals%d" % b, align_bytes=64) for b in range(BLOCKS)]
-        query_raw = held.tile([P, PACK, Q], F32, name="query_raw")
-        size_cols = held.tile([P, PACK], F32, name="size_cols")
+        query_raw = held.tile([P, PACK, Q], F32, name="query_raw", tag="query_raw")
+        size_rows = held.tile([P, P], F32, name="size_rows")
+        nc.vector.memset(size_rows[:], 0.0)
 
         keys_by_plane = keys.rearrange("(p t) n -> p t n", t=PACK)
         nc.sync.dma_start(key_planes[0][:], keys_by_plane[:, 0, :])
@@ -43,7 +44,7 @@ def tile_attend_smoothkeys_kernel(tc, query, keys, size, vals, offs, out):
         for t in range(1, PACK):
             nc.sync.dma_start(key_planes[t][:], keys_by_plane[:, t, :])
         nc.sync.dma_start(query_raw[:], query.rearrange("(p t) q -> p t q", t=PACK))
-        nc.sync.dma_start(size_cols[:], size.rearrange("o (p t) -> (o p) t", t=PACK))
+        nc.sync.dma_start(size_rows[: I // P, :], size.rearrange("o (j s) -> (o j) s", s=P))
         for b in (1, 0, 2, 3):
             nc.sync.dma_start(val_rows[b][:], vals[b * P : (b + 1) * P, :])
 
@@ -141,14 +142,17 @@ def tile_attend_smoothkeys_kernel(tc, query, keys, size, vals, offs, out):
         listed0 = gather_vals(0)
         inv_sum = held.tile([Q, 1], F32, name="inv_sum")
         nc.gpsimd.tensor_tensor(inv_sum[:], row_sum[:], minus_one[:], ALU.pow)
-        size_bank = psum.tile([P, PACK, P], F32, name="size_bank")
-        for t in range(PACK):
-            nc.tensor.transpose(size_bank[:, t, :], size_cols[:, t : t + 1].to_broadcast([P, P]), ident[:])
+        size_turned = psum.tile([P, P], F32, name="size_turned", tag="lead_acc")
+        nc.tensor.transpose(size_turned[:], size_rows[:], ident[:])
+        size_cols = held.tile([P, I // P], F32, name="size_cols", tag="query_raw")
+        nc.vector.tensor_copy(size_cols[:], size_turned[:, : I // P])
+        size_bank = psum.tile([P, I // P, P], F32, name="size_bank")
+        for j in range(I // P):
+            nc.tensor.transpose(size_bank[:, j, :], size_cols[:, j : j + 1].to_broadcast([P, P]), ident[:])
 
         w = held.tile([Q, I], BF16, name="w", tag="vals0", align_bytes=64)
         nc.vector.scalar_tensor_tensor(
-            w[:].rearrange("q (s t) -> q s t", t=PACK), p[:].rearrange("q (s t) -> q s t", t=PACK),
-            inv_sum[:], size_bank[:].rearrange("q t s -> q s t"), ALU.mult, ALU.mult,
+            w[:], p[:], inv_sum[:], size_bank[:].rearrange("q j s -> q (j s)"), ALU.mult, ALU.mult
         )
         turn_slots(listed0, lead[:, 0, :])
         turn_slots(w, lead[:, 1, :])
@@ -184,14 +188,15 @@ def tile_attend_smoothkeys_kernel(tc, query, keys, size, vals, offs, out):
             ("lead", slice(0, P), lead_codes[:, :P], lead_scales[:, :P]),
             ("pair", slice(P, 3 * P), pair_codes, pair_scales),
         ):
-            acc = psum.tile([Q, cols.stop - cols.start], F32, name=name + "_acc")
+            acc = psum.tile([Q, cols.stop - cols.start], F32, name=name + "_acc", tag=name + "_acc")
             multiply(acc[:], codes, scales)
             result = held.tile([Q, cols.stop - cols.start], F32, name=name + "_result")
             nc.scalar.copy(result[:], acc[:])
             nc.sync.dma_start(out[:, cols], result[:])
-        last_result = held.tile([Q, P], F32, name="last_result")
         for h, (codes, scales) in enumerate(last_parts):
             acc = turn.tile([Q, P // 2], F32, name="turned")
             multiply(acc[:], codes[:], scales[:])
-            nc.vector.tensor_copy(last_result[:, h * P // 2 : (h + 1) * P // 2], acc[:])
-        nc.sync.dma_start(out[:, 3 * P :], last_result[:])
+            result = held.tile([Q, P // 2], F32, name="last_result%d" % h)
+            nc.vector.tensor_copy(result[:], acc[:])
+            first_col = 3 * P + h * P // 2
+            nc.sync.dma_start(out[:, first_col : first_col + P // 2], result[:])

@@ -22,6 +22,7 @@ PAIRS = 2
 BLOCKS = E // P
 HALF = I // 2
 VECTOR_SLOTS = 256
+RUN = 16
 
 
 def tile_attend_smoothkeys_kernel(tc, query, keys, size, vals, offs, out):
@@ -63,15 +64,18 @@ def tile_attend_smoothkeys_kernel(tc, query, keys, size, vals, offs, out):
             words = rows[:].bitcast(F32)
             bank = turn.tile([P, PAIRS, P], F32, name="turned")
             for u in range(PAIRS):
-                nc.tensor.transpose(bank[:, u, :], words[:, u :: PAIRS], ident[:])
+                nc.tensor.transpose(bank[:, u, :], words[:, u * P : (u + 1) * P], ident[:])
             nc.scalar.copy(
                 grouped.bitcast(F32).rearrange("p (c u) -> p c u", u=PAIRS),
                 bank[:].rearrange("p u c -> p c u"),
             )
 
+        def by_runs(rows):
+            return rows.rearrange("p (u g r) -> p g u r", u=PAIRS, r=RUN)
+
         def gather_vals(b):
             rows = held.tile([P, I], BF16, name="listed_vals%d" % b, align_bytes=64)
-            nc.vector.tensor_copy(rows[:], val_rows[b][:].indirect(offsets[:]))
+            nc.vector.tensor_copy(by_runs(rows[:]), val_rows[b][:].indirect(offsets[:]))
             return rows
 
         km = held.tile([P, I, PACK], BF16, name="km", align_bytes=64)
@@ -136,7 +140,7 @@ def tile_attend_smoothkeys_kernel(tc, query, keys, size, vals, offs, out):
         row_sum = held.tile([Q, 1], F32, name="row_sum")
         nc.scalar.activation(p[:], scores[:], ACT.Exp, bias=neg_max[:], scale=1.0, accum_out=row_sum[:])
         listed1 = held.tile([P, I], BF16, name="listed_vals1", tag="neg_max", align_bytes=64)
-        nc.scalar.activation(listed1[:], first_pool[:].indirect(offsets[:]), ACT.Copy)
+        nc.scalar.activation(by_runs(listed1[:]), first_pool[:].indirect(offsets[:]), ACT.Copy)
         lead = held.tile([P, 2, P * PACK], BF16, name="lead", align_bytes=64)
         pair = held.tile([P, 2, P * PACK], BF16, name="pair", align_bytes=64)
         listed0 = gather_vals(0)
@@ -151,15 +155,19 @@ def tile_attend_smoothkeys_kernel(tc, query, keys, size, vals, offs, out):
             nc.tensor.transpose(size_bank[:, j, :], size_cols[:, j : j + 1].to_broadcast([P, P]), ident[:])
 
         w = held.tile([Q, I], BF16, name="w", tag="vals0", align_bytes=64)
-        nc.vector.scalar_tensor_tensor(
-            w[:], p[:], inv_sum[:], size_bank[:].rearrange("q j s -> q (j s)"), ALU.mult, ALU.mult
-        )
+        for u in range(PAIRS):
+            nc.vector.scalar_tensor_tensor(
+                w[:, u * HALF : (u + 1) * HALF].rearrange("q (g r) -> q g r", r=RUN),
+                p[:].rearrange("q (g u r) -> q u g r", u=PAIRS, r=RUN)[:, u],
+                inv_sum[:],
+                size_bank[:].rearrange("q j (g u r) -> q u (j g) r", u=PAIRS, r=RUN)[:, u],
+                ALU.mult, ALU.mult,
+            )
         turn_slots(listed0, lead[:, 0, :])
         turn_slots(w, lead[:, 1, :])
         turn_slots(listed1, pair[:, 0, :])
         turn_slots(gather_vals(2), pair[:, 1, :])
-        last_rows = held.tile([P, PAIRS, P, 2], BF16, name="last_rows", align_bytes=64)
-        nc.vector.tensor_copy(last_rows[:].rearrange("p u s e -> p s u e"), val_rows[3][:].indirect(offsets[:]))
+        last_rows = gather_vals(3)
         early_codes = held.tile([P, BLOCKS * P], U32, name="early_codes", tag="vals3", align_bytes=64)
         early_scales = held.tile([P, BLOCKS * P], U8, name="early_scales", align_bytes=64)
         lead_codes, lead_scales = early_codes[:, : 2 * P], early_scales[:, : 2 * P]
@@ -168,7 +176,7 @@ def tile_attend_smoothkeys_kernel(tc, query, keys, size, vals, offs, out):
             nc.vector.quantize_mx(out=codes.bitcast(FP8X4), scales=scales, in_=grouped[:].rearrange("p b c -> p (b c)"))
         last_bank = turn.tile([P, PAIRS, P], F32, name="turned")
         for u in range(PAIRS):
-            nc.tensor.transpose(last_bank[:, u, :], last_rows[:, u, :, :].rearrange("p s e -> p (s e)").bitcast(F32), ident[:])
+            nc.tensor.transpose(last_bank[:, u, :], last_rows[:].bitcast(F32)[:, u * P : (u + 1) * P], ident[:])
         last_parts = []
         for h in range(2):
             part = held.tile([P, P * PACK // 2], BF16, name="last%d" % h, align_bytes=64)

@@ -23,6 +23,7 @@ BLOCKS = E // P
 HALF = I // 2
 VECTOR_SLOTS = 256
 RUN = 16
+LAST_SPLIT = 320
 
 
 def tile_attend_smoothkeys_kernel(tc, query, keys, size, vals, offs, out):
@@ -108,7 +109,7 @@ def tile_attend_smoothkeys_kernel(tc, query, keys, size, vals, offs, out):
             accum_out=neg_mean[:, last:],
         )
         nc.scalar.activation(
-            km[:, VECTOR_SLOTS:, last], listed[:, last, VECTOR_SLOTS:], ACT.Identity, bias=neg_mean[:, last:], scale=1.0
+            km[:, LAST_SPLIT:, last], listed[:, last, LAST_SPLIT:], ACT.Identity, bias=neg_mean[:, last:], scale=1.0
         )
         nc.vector.tensor_copy(query_grouped[:], query_raw[:].rearrange("p t q -> p q t"))
         q_codes, q_scales = quantise("query", query_grouped[:].rearrange("p q t -> p (q t)"), Q, "query_codes")
@@ -118,16 +119,20 @@ def tile_attend_smoothkeys_kernel(tc, query, keys, size, vals, offs, out):
             neg_mean[:, 2:].unsqueeze(1).to_broadcast([P, VECTOR_SLOTS, 2]),
             ALU.add,
         )
+        nc.vector.tensor_scalar(
+            km[:, VECTOR_SLOTS:LAST_SPLIT, last], listed[:, last, VECTOR_SLOTS:LAST_SPLIT], neg_mean[:, last:], None, ALU.add
+        )
+        pieces = (slice(3 * P, I), slice(0, 2 * P), slice(2 * P, 3 * P))
         km_codes = held.tile([P, I], U32, name="km_codes", align_bytes=64)
         km_scales = held.tile([P, I], U8, name="km_scales", align_bytes=64)
-        for cols in (slice(VECTOR_SLOTS, I), slice(0, VECTOR_SLOTS)):
+        for cols in pieces:
             nc.vector.quantize_mx(
                 out=km_codes[:, cols].bitcast(FP8X4), scales=km_scales[:, cols],
                 in_=km[:, cols, :].rearrange("p i t -> p (i t)"),
             )
 
         scores = psum.tile([Q, I], F32, name="scores")
-        for cols in (slice(VECTOR_SLOTS, I), slice(0, VECTOR_SLOTS)):
+        for cols in pieces:
             nc.tensor.matmul_mx(
                 out=scores[:, cols], lhsT=q_codes[:].bitcast(FP8X4), lhsT_scale=q_scales[:],
                 rhs=km_codes[:, cols].bitcast(FP8X4), rhs_scale=km_scales[:, cols], start=True, stop=True,

@@ -21,195 +21,198 @@ PACK = 4
 PAIRS = 2
 BLOCKS = E // P
 HALF = I // 2
-VECTOR_SLOTS = 256
-RUN = 16
-LAST_SPLIT = 320
+STRIPE = 16
+VECTOR_GATHER = 256
+VECTOR_CENTRE = 416
+KIB = 1024
 
 
 def tile_attend_smoothkeys_kernel(tc, query, keys, size, vals, offs, out):
     nc = tc.nc
     with ExitStack() as ctx:
         held = ctx.enter_context(tc.tile_pool(name="held", bufs=1))
+        placed = ctx.enter_context(tc.tile_pool(name="placed", bufs=1))
         psum = ctx.enter_context(tc.psum_pool(name="psum", bufs=1))
         turn = ctx.enter_context(tc.psum_pool(name="turn", bufs=3))
 
-        offsets = held.tile([P, I // 16], U16, name="offsets")
-        key_planes = [held.tile([P, T], F32, name="keys%d" % t) for t in range(PACK)]
-        val_rows = [held.tile([P, T], F32, name="vals%d" % b, tag="vals%d" % b, align_bytes=64) for b in range(BLOCKS)]
-        query_raw = held.tile([P, PACK, Q], F32, name="query_raw", tag="query_raw")
+        def place(name, shape, dtype, offset):
+            return placed.tile(shape, dtype, name=name, offset=offset, align_bytes=64)
+
+        offsets = held.tile([P, I // STRIPE], U16, name="offsets")
+        on_keys0 = BLOCKS * 8 * KIB
+        key_planes = [place("keys0", [P, T], F32, on_keys0)]
+        key_planes.extend(held.tile([P, T], F32, name="keys%d" % t) for t in range(1, PACK))
+        on_vals = [b * 8 * KIB for b in range(BLOCKS)]
+        val_rows = [place("vals%d" % b, [P, T], F32, on_vals[b]) for b in range(BLOCKS)]
+        query_raw = held.tile([P, PACK, Q], F32, name="query_raw")
         size_rows = held.tile([P, P], F32, name="size_rows")
-        nc.vector.memset(size_rows[:], 0.0)
+        nc.gpsimd.memset(size_rows[:], 0.0)
 
         keys_by_plane = keys.rearrange("(p t) n -> p t n", t=PACK)
         nc.sync.dma_start(key_planes[0][:], keys_by_plane[:, 0, :])
         nc.sync.dma_start(offsets[:], offs)
+        nc.sync.dma_start(size_rows[: I // P, :], size.rearrange("o (j s) -> (o j) s", s=P))
         for t in range(1, PACK):
             nc.sync.dma_start(key_planes[t][:], keys_by_plane[:, t, :])
         nc.sync.dma_start(query_raw[:], query.rearrange("(p t) q -> p t q", t=PACK))
-        nc.sync.dma_start(size_rows[: I // P, :], size.rearrange("o (j s) -> (o j) s", s=P))
-        for b in (1, 0, 2, 3):
+        for b in range(BLOCKS):
             nc.sync.dma_start(val_rows[b][:], vals[b * P : (b + 1) * P, :])
 
         ident = held.tile([P, P], F32, name="ident")
         make_identity(nc, ident[:])
-        minus_one = held.tile([Q, 1], F32, name="minus_one")
-        nc.gpsimd.memset(minus_one[:], -1.0)
+        mean_scale = held.tile([P, 1], F32, name="mean_scale")
+        one = held.tile([Q, 1], F32, name="one")
+        nc.gpsimd.memset(one[:], 1.0)
+        nc.scalar.activation(mean_scale[:], one[:], ACT.Identity, scale=-1.0 / I)
 
-        def quantise(name, grouped, width, tag):
-            codes = held.tile([P, width], U32, name=name + "_codes", tag=tag, align_bytes=64)
-            scales = held.tile([P, width], U8, name=name + "_scales", align_bytes=64)
-            nc.vector.quantize_mx(out=codes[:].bitcast(FP8X4), scales=scales[:], in_=grouped)
-            return codes, scales
+        def gather_on_vector(rows, window, first, stop):
+            nc.vector.tensor_copy(rows[:, first:stop], window.indirect(offsets[:, first // STRIPE : stop // STRIPE]))
 
-        def turn_slots(rows, grouped):
-            words = rows[:].bitcast(F32)
+        def gather_on_scalar(rows, window, first, stop):
+            nc.scalar.activation(
+                rows[:, first:stop], window.indirect(offsets[:, first // STRIPE : stop // STRIPE]), ACT.Copy
+            )
+
+        def gather_shared(rows, window, split):
+            gather_on_vector(rows, window, 0, split)
+            gather_on_scalar(rows, window, split, I)
+
+        def quantise(codes, scales, grouped):
+            nc.vector.quantize_mx(out=codes.bitcast(FP8X4), scales=scales, in_=grouped)
+
+        def turn_slots(rows):
+            words = rows.bitcast(F32)
             bank = turn.tile([P, PAIRS, P], F32, name="turned")
             for u in range(PAIRS):
-                nc.tensor.transpose(bank[:, u, :], words[:, u * P : (u + 1) * P], ident[:])
-            nc.scalar.copy(
-                grouped.bitcast(F32).rearrange("p (c u) -> p c u", u=PAIRS),
-                bank[:].rearrange("p u c -> p c u"),
-            )
+                nc.tensor.transpose(bank[:, u, :], words[:, u : HALF : PAIRS], ident[:])
+            return bank
 
-        def by_runs(rows):
-            return rows.rearrange("p (u g r) -> p g u r", u=PAIRS, r=RUN)
+        def as_words(grouped):
+            return grouped.bitcast(F32).rearrange("p (c u) -> p c u", u=PAIRS)
 
-        def gather_vals(b):
-            rows = held.tile([P, I], BF16, name="listed_vals%d" % b, align_bytes=64)
-            nc.vector.tensor_copy(by_runs(rows[:]), val_rows[b][:].indirect(offsets[:]))
-            return rows
+        def by_columns(bank):
+            return bank.rearrange("p u c -> p c u")
 
         km = held.tile([P, I, PACK], BF16, name="km", align_bytes=64)
-        query_grouped = held.tile([P, Q, PACK], BF16, name="query_grouped", align_bytes=64)
         listed = held.tile([P, PACK, I], F32, name="listed_keys")
+        scaled = held.tile([P, PACK, I], BF16, name="scaled_keys")
+        neg_part = held.tile([P, PACK, 2], F32, name="neg_part")
         neg_mean = held.tile([P, PACK], F32, name="neg_mean")
-        part_mean = held.tile([P, 1], F32, name="part_mean")
-        scaled = held.tile([P, I], BF16, name="scaled_keys")
+        halves = (slice(0, HALF), slice(HALF, I))
         last = PACK - 1
-        for t in range(last):
-            nc.vector.tensor_copy(listed[:, t, :], key_planes[t][:].indirect(offsets[:]))
+        for t in range(PACK):
+            gather_shared(listed[:, t, :], key_planes[t][:], HALF)
             nc.vector.tensor_scalar(
-                scaled[:], listed[:, t, :], -1.0 / I, None, ALU.mult, ALU.add, accum_out=neg_mean[:, t : t + 1]
+                scaled[:, t, :HALF], listed[:, t, :HALF], -1.0 / I, None, ALU.mult, ALU.add,
+                accum_out=neg_part[:, t, 0:1],
             )
-            split = VECTOR_SLOTS if t >= 2 else 0
             nc.scalar.activation(
-                km[:, split:, t], listed[:, t, split:], ACT.Identity, bias=neg_mean[:, t : t + 1], scale=1.0
+                scaled[:, t, HALF:], listed[:, t, HALF:], ACT.Copy, scale=mean_scale[:], accum_out=neg_part[:, t, 1:2]
             )
-        for h in range(2):
-            nc.vector.tensor_copy(
-                listed[:, last, h * HALF : (h + 1) * HALF],
-                key_planes[last][:].indirect(offsets[:, h * HALF // 16 : (h + 1) * HALF // 16]),
+            nc.scalar.activation(
+                neg_mean[:, t : t + 1], neg_part[:, t, 0:1], ACT.Identity, bias=neg_part[:, t, 1:2], scale=1.0
             )
-        scaled_last = held.tile([P, I], BF16, name="scaled_last")
-        nc.scalar.activation(
-            scaled_last[:, :HALF], listed[:, last, :HALF], ACT.Copy, scale=-1.0 / (I * HALF), accum_out=part_mean[:]
-        )
-        nc.scalar.activation(
-            scaled_last[:, HALF:], listed[:, last, HALF:], ACT.Identity, bias=part_mean[:], scale=-1.0 / I,
-            accum_out=neg_mean[:, last:],
-        )
-        nc.scalar.activation(
-            km[:, LAST_SPLIT:, last], listed[:, last, LAST_SPLIT:], ACT.Identity, bias=neg_mean[:, last:], scale=1.0
-        )
-        nc.vector.tensor_copy(query_grouped[:], query_raw[:].rearrange("p t q -> p q t"))
-        q_codes, q_scales = quantise("query", query_grouped[:].rearrange("p q t -> p (q t)"), Q, "query_codes")
-        nc.vector.tensor_tensor(
-            km[:, :VECTOR_SLOTS, 2:],
-            listed[:, 2:, :VECTOR_SLOTS].rearrange("p t i -> p i t"),
-            neg_mean[:, 2:].unsqueeze(1).to_broadcast([P, VECTOR_SLOTS, 2]),
-            ALU.add,
-        )
-        nc.vector.tensor_scalar(
-            km[:, VECTOR_SLOTS:LAST_SPLIT, last], listed[:, last, VECTOR_SLOTS:LAST_SPLIT], neg_mean[:, last:], None, ALU.add
-        )
-        pieces = (slice(3 * P, I), slice(0, 2 * P), slice(2 * P, 3 * P))
+            nc.scalar.activation(
+                km[:, VECTOR_CENTRE:, t], listed[:, t, VECTOR_CENTRE:], ACT.Identity,
+                bias=neg_mean[:, t : t + 1], scale=1.0,
+            )
+            for cols in (slice(0, HALF), slice(HALF, VECTOR_CENTRE)) if t == last else (slice(0, VECTOR_CENTRE),):
+                nc.vector.tensor_scalar(
+                    km[:, cols, t], listed[:, t, cols], neg_part[:, t, 0:1], neg_part[:, t, 1:2], ALU.add, ALU.add
+                )
+        query_grouped = held.tile([P, Q, PACK], BF16, name="query_grouped", align_bytes=64)
+        nc.scalar.copy(query_grouped[:], query_raw[:].rearrange("p t q -> p q t"))
+        size_turned = psum.tile([P, P], F32, name="size_turned", tag="early_acc")
+        nc.tensor.transpose(size_turned[:], size_rows[:], ident[:])
+        size_cols = place("size_cols", [P, I // P], F32, on_keys0)
+        nc.scalar.copy(size_cols[:], size_turned[:, : I // P])
+        size_bank = psum.tile([P, I // P, P], F32, name="size_bank", tag="size_bank")
+        for j in range(I // P):
+            nc.tensor.transpose(size_bank[:, j, :], size_cols[:, j : j + 1].to_broadcast([P, P]), ident[:])
+        q_codes = held.tile([P, Q], U32, name="q_codes", align_bytes=64)
+        q_scales = held.tile([P, Q], U8, name="q_scales", align_bytes=64)
+        quantise(q_codes[:], q_scales[:], query_grouped[:].rearrange("p q t -> p (q t)"))
         km_codes = held.tile([P, I], U32, name="km_codes", align_bytes=64)
         km_scales = held.tile([P, I], U8, name="km_scales", align_bytes=64)
-        for cols in pieces:
-            nc.vector.quantize_mx(
-                out=km_codes[:, cols].bitcast(FP8X4), scales=km_scales[:, cols],
-                in_=km[:, cols, :].rearrange("p i t -> p (i t)"),
-            )
-
-        scores = psum.tile([Q, I], F32, name="scores")
-        for cols in pieces:
+        scores = psum.tile([Q, I], F32, name="scores", tag="scores")
+        for cols in halves:
+            quantise(km_codes[:, cols], km_scales[:, cols], km[:, cols, :].rearrange("p i t -> p (i t)"))
+        for cols in halves:
             nc.tensor.matmul_mx(
                 out=scores[:, cols], lhsT=q_codes[:].bitcast(FP8X4), lhsT_scale=q_scales[:],
                 rhs=km_codes[:, cols].bitcast(FP8X4), rhs_scale=km_scales[:, cols], start=True, stop=True,
             )
-        first_pool = held.tile([P, T], BF16, name="first_pool", align_bytes=64)
-        nc.scalar.activation(first_pool[:], val_rows[1][:], ACT.Copy)
-        neg_max = held.tile([Q, 1], F32, name="neg_max", tag="neg_max", align_bytes=64)
+
+        listed_vals = [held.tile([P, I], BF16, name="listed_vals%d" % b, align_bytes=64) for b in range(BLOCKS)]
+        gather_on_scalar(listed_vals[0][:], val_rows[0][:], 0, I)
+        neg_max = held.tile([Q, 1], F32, name="neg_max")
         nc.vector.tensor_reduce(neg_max[:], scores[:], AXIS.X, ALU.max, negate=True)
-        p = held.tile([Q, I], F32, name="p", tag="vals1", align_bytes=64)
+        p = place("p", [Q, I], F32, on_vals[0])
         row_sum = held.tile([Q, 1], F32, name="row_sum")
         nc.scalar.activation(p[:], scores[:], ACT.Exp, bias=neg_max[:], scale=1.0, accum_out=row_sum[:])
-        listed1 = held.tile([P, I], BF16, name="listed_vals1", tag="neg_max", align_bytes=64)
-        nc.scalar.activation(by_runs(listed1[:]), first_pool[:].indirect(offsets[:]), ACT.Copy)
-        lead = held.tile([P, 2, P * PACK], BF16, name="lead", align_bytes=64)
-        pair = held.tile([P, 2, P * PACK], BF16, name="pair", align_bytes=64)
-        listed0 = gather_vals(0)
         inv_sum = held.tile([Q, 1], F32, name="inv_sum")
-        nc.gpsimd.tensor_tensor(inv_sum[:], row_sum[:], minus_one[:], ALU.pow)
-        size_turned = psum.tile([P, P], F32, name="size_turned", tag="lead_acc")
-        nc.tensor.transpose(size_turned[:], size_rows[:], ident[:])
-        size_cols = held.tile([P, I // P], F32, name="size_cols", tag="query_raw")
-        nc.vector.tensor_copy(size_cols[:], size_turned[:, : I // P])
-        size_bank = psum.tile([P, I // P, P], F32, name="size_bank")
-        for j in range(I // P):
-            nc.tensor.transpose(size_bank[:, j, :], size_cols[:, j : j + 1].to_broadcast([P, P]), ident[:])
-
-        w = held.tile([Q, I], BF16, name="w", tag="vals0", align_bytes=64)
-        for u in range(PAIRS):
-            nc.vector.scalar_tensor_tensor(
-                w[:, u * HALF : (u + 1) * HALF].rearrange("q (g r) -> q g r", r=RUN),
-                p[:].rearrange("q (g u r) -> q u g r", u=PAIRS, r=RUN)[:, u],
-                inv_sum[:],
-                size_bank[:].rearrange("q j (g u r) -> q u (j g) r", u=PAIRS, r=RUN)[:, u],
-                ALU.mult, ALU.mult,
-            )
-        turn_slots(listed0, lead[:, 0, :])
-        turn_slots(w, lead[:, 1, :])
-        turn_slots(listed1, pair[:, 0, :])
-        turn_slots(gather_vals(2), pair[:, 1, :])
-        last_rows = gather_vals(3)
-        early_codes = held.tile([P, BLOCKS * P], U32, name="early_codes", tag="vals3", align_bytes=64)
-        early_scales = held.tile([P, BLOCKS * P], U8, name="early_scales", align_bytes=64)
-        lead_codes, lead_scales = early_codes[:, : 2 * P], early_scales[:, : 2 * P]
-        pair_codes, pair_scales = early_codes[:, 2 * P :], early_scales[:, 2 * P :]
-        for codes, scales, grouped in ((lead_codes, lead_scales, lead), (pair_codes, pair_scales, pair)):
-            nc.vector.quantize_mx(out=codes.bitcast(FP8X4), scales=scales, in_=grouped[:].rearrange("p b c -> p (b c)"))
-        last_bank = turn.tile([P, PAIRS, P], F32, name="turned")
-        for u in range(PAIRS):
-            nc.tensor.transpose(last_bank[:, u, :], last_rows[:].bitcast(F32)[:, u * P : (u + 1) * P], ident[:])
-        last_parts = []
-        for h in range(2):
-            part = held.tile([P, P * PACK // 2], BF16, name="last%d" % h, align_bytes=64)
-            nc.scalar.copy(
-                part[:].bitcast(F32).rearrange("p (c u) -> p c u", u=PAIRS),
-                last_bank[:, :, h * P // 2 : (h + 1) * P // 2].rearrange("p u c -> p c u"),
-            )
-            last_parts.append(quantise("last%d" % h, part[:], P // 2, "last_codes%d" % h))
+        nc.vector.reciprocal(inv_sum[:], row_sum[:])
+        bank0 = turn_slots(listed_vals[0][:])
+        grouped0 = held.tile([P, P * PACK], BF16, name="grouped0", align_bytes=64)
+        nc.vector.tensor_copy(as_words(grouped0[:]), by_columns(bank0[:]))
+        v_codes = held.tile([P, 2 * P], U32, name="v_codes", align_bytes=64)
+        v_scales = held.tile([P, 2 * P], U8, name="v_scales", align_bytes=64)
+        quantise(v_codes[:, :P], v_scales[:, :P], grouped0[:])
+        gather_on_scalar(listed_vals[1][:], val_rows[1][:], 0, I)
+        w = held.tile([Q, I], BF16, name="w", align_bytes=64)
+        nc.vector.scalar_tensor_tensor(
+            w[:], p[:], inv_sum[:], size_bank[:].rearrange("q j s -> q (j s)"), ALU.mult, ALU.mult
+        )
+        w_bank = turn_slots(w[:])
+        bank1 = turn_slots(listed_vals[1][:])
+        gather_shared(listed_vals[2][:], val_rows[2][:], VECTOR_GATHER)
+        grouped1 = place("grouped1", [P, P * PACK], BF16, on_vals[2] + KIB)
+        nc.vector.tensor_copy(as_words(grouped1[:]), by_columns(bank1[:]))
+        w_grouped = place("w_grouped", [P, Q * PACK], BF16, on_vals[2])
+        nc.scalar.copy(as_words(w_grouped[:]), by_columns(w_bank[:]))
+        w_codes = held.tile([P, Q], U32, name="w_codes", align_bytes=64)
+        w_scales = held.tile([P, Q], U8, name="w_scales", align_bytes=64)
+        quantise(w_codes[:], w_scales[:], w_grouped[:])
+        quantise(v_codes[:, P:], v_scales[:, P:], grouped1[:])
 
         def multiply(acc, codes, scales):
             nc.tensor.matmul_mx(
-                out=acc, lhsT=lead_codes[:, P:].bitcast(FP8X4), lhsT_scale=lead_scales[:, P:],
+                out=acc, lhsT=w_codes[:].bitcast(FP8X4), lhsT_scale=w_scales[:],
                 rhs=codes.bitcast(FP8X4), rhs_scale=scales, start=True, stop=True,
             )
 
-        for name, cols, codes, scales in (
-            ("lead", slice(0, P), lead_codes[:, :P], lead_scales[:, :P]),
-            ("pair", slice(P, 3 * P), pair_codes, pair_scales),
-        ):
-            acc = psum.tile([Q, cols.stop - cols.start], F32, name=name + "_acc", tag=name + "_acc")
-            multiply(acc[:], codes, scales)
-            result = held.tile([Q, cols.stop - cols.start], F32, name=name + "_result")
-            nc.scalar.copy(result[:], acc[:])
-            nc.sync.dma_start(out[:, cols], result[:])
+        bank2 = turn_slots(listed_vals[2][:])
+        early_acc = psum.tile([Q, 2 * P], F32, name="early_acc", tag="early_acc")
+        multiply(early_acc[:], v_codes[:], v_scales[:])
+        grouped2 = held.tile([P, P * PACK], BF16, name="grouped2", align_bytes=64)
+        nc.scalar.copy(as_words(grouped2[:]), by_columns(bank2[:]))
+
+        gather_shared(listed_vals[3][:], val_rows[3][:], VECTOR_GATHER)
+        early_result = place("early_result", [Q, 2 * P], F32, on_vals[3])
+        nc.scalar.copy(early_result[:], early_acc[:])
+        nc.sync.dma_start(out[:, : 2 * P], early_result[:])
+        codes2 = place("codes2", [P, P], U32, on_vals[3] + KIB)
+        scales2 = held.tile([P, P], U8, name="scales2", align_bytes=64)
+        quantise(codes2[:], scales2[:], grouped2[:])
+        last_bank = turn_slots(listed_vals[3][:])
+        third_acc = psum.tile([Q, P], F32, name="third_acc")
+        multiply(third_acc[:], codes2[:], scales2[:])
+        width = P // 2
+        last_parts = []
+        for h in range(2):
+            part = held.tile([P, width * PACK], BF16, name="last%d" % h, align_bytes=64)
+            nc.scalar.copy(as_words(part[:]), by_columns(last_bank[:, :, h * width : (h + 1) * width]))
+            codes = held.tile([P, width], U32, name="last_codes%d" % h, align_bytes=64)
+            scales = held.tile([P, width], U8, name="last_scales%d" % h, align_bytes=64)
+            quantise(codes[:], scales[:], part[:])
+            last_parts.append((codes, scales))
+        third_result = held.tile([Q, P], F32, name="third_result")
+        nc.scalar.copy(third_result[:], third_acc[:])
+        nc.sync.dma_start(out[:, 2 * P : 3 * P], third_result[:])
         for h, (codes, scales) in enumerate(last_parts):
-            acc = turn.tile([Q, P // 2], F32, name="turned")
+            acc = psum.tile([Q, width], F32, name="last_acc%d" % h, tag=("scores", "size_bank")[h])
             multiply(acc[:], codes[:], scales[:])
-            result = held.tile([Q, P // 2], F32, name="last_result%d" % h)
+            result = held.tile([Q, width], F32, name="last_result%d" % h)
             nc.vector.tensor_copy(result[:], acc[:])
-            first_col = 3 * P + h * P // 2
-            nc.sync.dma_start(out[:, first_col : first_col + P // 2], result[:])
+            first_col = 3 * P + h * width
+            nc.sync.dma_start(out[:, first_col : first_col + width], result[:])

@@ -170,10 +170,18 @@ def tile_attend_smoothkeys_kernel(tc, query, keys, size, vals, offs, out):
         nc.vector.tensor_copy(as_words(grouped1[:]), by_columns(bank1[:]))
         w_grouped = place("w_grouped", [P, Q * PACK], BF16, on_vals[2])
         nc.scalar.copy(as_words(w_grouped[:]), by_columns(w_bank[:]))
-        w_codes = held.tile([P, Q], U32, name="w_codes", align_bytes=64)
+        quantise(v_codes[:, P:], v_scales[:, P:], grouped1[:])
+        bank2 = turn_slots(listed_vals[2][:])
+
+        gather_shared(listed_vals[3][:], val_rows[3][:], VECTOR_GATHER)
+        w_codes = place("w_codes", [P, Q], U32, on_vals[3])
         w_scales = held.tile([P, Q], U8, name="w_scales", align_bytes=64)
         quantise(w_codes[:], w_scales[:], w_grouped[:])
-        quantise(v_codes[:, P:], v_scales[:, P:], grouped1[:])
+        grouped2 = place("grouped2", [P, P * PACK], BF16, on_vals[3] + KIB)
+        nc.scalar.copy(as_words(grouped2[:]), by_columns(bank2[:]))
+        codes2 = held.tile([P, P], U32, name="codes2", align_bytes=64)
+        scales2 = held.tile([P, P], U8, name="scales2", align_bytes=64)
+        quantise(codes2[:], scales2[:], grouped2[:])
 
         def multiply(acc, codes, scales):
             nc.tensor.matmul_mx(
@@ -181,20 +189,9 @@ def tile_attend_smoothkeys_kernel(tc, query, keys, size, vals, offs, out):
                 rhs=codes.bitcast(FP8X4), rhs_scale=scales, start=True, stop=True,
             )
 
-        bank2 = turn_slots(listed_vals[2][:])
+        last_bank = turn_slots(listed_vals[3][:])
         early_acc = psum.tile([Q, 2 * P], F32, name="early_acc", tag="early_acc")
         multiply(early_acc[:], v_codes[:], v_scales[:])
-        grouped2 = held.tile([P, P * PACK], BF16, name="grouped2", align_bytes=64)
-        nc.scalar.copy(as_words(grouped2[:]), by_columns(bank2[:]))
-
-        gather_shared(listed_vals[3][:], val_rows[3][:], VECTOR_GATHER)
-        early_result = place("early_result", [Q, 2 * P], F32, on_vals[3])
-        nc.scalar.copy(early_result[:], early_acc[:])
-        nc.sync.dma_start(out[:, : 2 * P], early_result[:])
-        codes2 = place("codes2", [P, P], U32, on_vals[3] + KIB)
-        scales2 = held.tile([P, P], U8, name="scales2", align_bytes=64)
-        quantise(codes2[:], scales2[:], grouped2[:])
-        last_bank = turn_slots(listed_vals[3][:])
         third_acc = psum.tile([Q, P], F32, name="third_acc")
         multiply(third_acc[:], codes2[:], scales2[:])
         width = P // 2
@@ -206,6 +203,9 @@ def tile_attend_smoothkeys_kernel(tc, query, keys, size, vals, offs, out):
             scales = held.tile([P, width], U8, name="last_scales%d" % h, align_bytes=64)
             quantise(codes[:], scales[:], part[:])
             last_parts.append((codes, scales))
+        early_result = held.tile([Q, 2 * P], F32, name="early_result")
+        nc.scalar.copy(early_result[:], early_acc[:])
+        nc.sync.dma_start(out[:, : 2 * P], early_result[:])
         third_result = held.tile([Q, P], F32, name="third_result")
         nc.scalar.copy(third_result[:], third_acc[:])
         nc.sync.dma_start(out[:, 2 * P : 3 * P], third_result[:])

@@ -22,8 +22,9 @@ PAIRS = 2
 BLOCKS = E // P
 HALF = I // 2
 STRIPE = 16
-VECTOR_GATHER = 256
-VECTOR_CENTRE = 416
+THIRD_VECTOR_GATHER = 320
+VECTOR_SLOTS = 256
+LAST_SPLIT = 320
 KIB = 1024
 
 
@@ -39,31 +40,27 @@ def tile_attend_smoothkeys_kernel(tc, query, keys, size, vals, offs, out):
             return placed.tile(shape, dtype, name=name, offset=offset, align_bytes=64)
 
         offsets = held.tile([P, I // STRIPE], U16, name="offsets")
-        on_keys0 = BLOCKS * 8 * KIB
-        key_planes = [place("keys0", [P, T], F32, on_keys0)]
-        key_planes.extend(held.tile([P, T], F32, name="keys%d" % t) for t in range(1, PACK))
+        key_planes = [held.tile([P, T], F32, name="keys%d" % t) for t in range(PACK)]
         on_vals = [b * 8 * KIB for b in range(BLOCKS)]
         val_rows = [place("vals%d" % b, [P, T], F32, on_vals[b]) for b in range(BLOCKS)]
-        query_raw = held.tile([P, PACK, Q], F32, name="query_raw")
+        query_raw = held.tile([P, PACK, Q], F32, name="query_raw", tag="query_raw")
         size_rows = held.tile([P, P], F32, name="size_rows")
-        nc.gpsimd.memset(size_rows[:], 0.0)
+        nc.vector.memset(size_rows[:], 0.0)
 
         keys_by_plane = keys.rearrange("(p t) n -> p t n", t=PACK)
         nc.sync.dma_start(key_planes[0][:], keys_by_plane[:, 0, :])
         nc.sync.dma_start(offsets[:], offs)
-        nc.sync.dma_start(size_rows[: I // P, :], size.rearrange("o (j s) -> (o j) s", s=P))
         for t in range(1, PACK):
             nc.sync.dma_start(key_planes[t][:], keys_by_plane[:, t, :])
         nc.sync.dma_start(query_raw[:], query.rearrange("(p t) q -> p t q", t=PACK))
+        nc.sync.dma_start(size_rows[: I // P, :], size.rearrange("o (j s) -> (o j) s", s=P))
         for b in range(BLOCKS):
             nc.sync.dma_start(val_rows[b][:], vals[b * P : (b + 1) * P, :])
 
         ident = held.tile([P, P], F32, name="ident")
         make_identity(nc, ident[:])
-        mean_scale = held.tile([P, 1], F32, name="mean_scale")
-        one = held.tile([Q, 1], F32, name="one")
-        nc.gpsimd.memset(one[:], 1.0)
-        nc.scalar.activation(mean_scale[:], one[:], ACT.Identity, scale=-1.0 / I)
+        minus_one = held.tile([Q, 1], F32, name="minus_one")
+        nc.gpsimd.memset(minus_one[:], -1.0)
 
         def gather_on_vector(rows, window, first, stop):
             nc.vector.tensor_copy(rows[:, first:stop], window.indirect(offsets[:, first // STRIPE : stop // STRIPE]))
@@ -94,55 +91,65 @@ def tile_attend_smoothkeys_kernel(tc, query, keys, size, vals, offs, out):
             return bank.rearrange("p u c -> p c u")
 
         km = held.tile([P, I, PACK], BF16, name="km", align_bytes=64)
-        listed = held.tile([P, PACK, I], F32, name="listed_keys")
-        scaled = held.tile([P, PACK, I], BF16, name="scaled_keys")
-        neg_part = held.tile([P, PACK, 2], F32, name="neg_part")
-        neg_mean = held.tile([P, PACK], F32, name="neg_mean")
-        halves = (slice(0, HALF), slice(HALF, I))
-        last = PACK - 1
-        for t in range(PACK):
-            gather_shared(listed[:, t, :], key_planes[t][:], HALF)
-            nc.vector.tensor_scalar(
-                scaled[:, t, :HALF], listed[:, t, :HALF], -1.0 / I, None, ALU.mult, ALU.add,
-                accum_out=neg_part[:, t, 0:1],
-            )
-            nc.scalar.activation(
-                scaled[:, t, HALF:], listed[:, t, HALF:], ACT.Copy, scale=mean_scale[:], accum_out=neg_part[:, t, 1:2]
-            )
-            nc.scalar.activation(
-                neg_mean[:, t : t + 1], neg_part[:, t, 0:1], ACT.Identity, bias=neg_part[:, t, 1:2], scale=1.0
-            )
-            nc.scalar.activation(
-                km[:, VECTOR_CENTRE:, t], listed[:, t, VECTOR_CENTRE:], ACT.Identity,
-                bias=neg_mean[:, t : t + 1], scale=1.0,
-            )
-            for cols in (slice(0, HALF), slice(HALF, VECTOR_CENTRE)) if t == last else (slice(0, VECTOR_CENTRE),):
-                nc.vector.tensor_scalar(
-                    km[:, cols, t], listed[:, t, cols], neg_part[:, t, 0:1], neg_part[:, t, 1:2], ALU.add, ALU.add
-                )
         query_grouped = held.tile([P, Q, PACK], BF16, name="query_grouped", align_bytes=64)
-        nc.scalar.copy(query_grouped[:], query_raw[:].rearrange("p t q -> p q t"))
-        size_turned = psum.tile([P, P], F32, name="size_turned", tag="early_acc")
-        nc.tensor.transpose(size_turned[:], size_rows[:], ident[:])
-        size_cols = place("size_cols", [P, I // P], F32, on_keys0)
-        nc.scalar.copy(size_cols[:], size_turned[:, : I // P])
-        size_bank = psum.tile([P, I // P, P], F32, name="size_bank", tag="size_bank")
-        for j in range(I // P):
-            nc.tensor.transpose(size_bank[:, j, :], size_cols[:, j : j + 1].to_broadcast([P, P]), ident[:])
+        listed = held.tile([P, PACK, I], F32, name="listed_keys")
+        neg_mean = held.tile([P, PACK], F32, name="neg_mean")
+        part_mean = held.tile([P, 1], F32, name="part_mean")
+        scaled = held.tile([P, I], BF16, name="scaled_keys")
+        last = PACK - 1
+        for t in range(last):
+            nc.vector.tensor_copy(listed[:, t, :], key_planes[t][:].indirect(offsets[:]))
+            nc.vector.tensor_scalar(
+                scaled[:], listed[:, t, :], -1.0 / I, None, ALU.mult, ALU.add, accum_out=neg_mean[:, t : t + 1]
+            )
+            split = VECTOR_SLOTS if t >= 2 else 0
+            nc.scalar.activation(
+                km[:, split:, t], listed[:, t, split:], ACT.Identity, bias=neg_mean[:, t : t + 1], scale=1.0
+            )
+        for h in range(2):
+            nc.vector.tensor_copy(
+                listed[:, last, h * HALF : (h + 1) * HALF],
+                key_planes[last][:].indirect(offsets[:, h * HALF // 16 : (h + 1) * HALF // 16]),
+            )
+        scaled_last = held.tile([P, I], BF16, name="scaled_last")
+        nc.scalar.activation(
+            scaled_last[:, :HALF], listed[:, last, :HALF], ACT.Copy, scale=-1.0 / (I * HALF), accum_out=part_mean[:]
+        )
+        nc.scalar.activation(
+            scaled_last[:, HALF:], listed[:, last, HALF:], ACT.Identity, bias=part_mean[:], scale=-1.0 / I,
+            accum_out=neg_mean[:, last:],
+        )
+        nc.scalar.activation(
+            km[:, LAST_SPLIT:, last], listed[:, last, LAST_SPLIT:], ACT.Identity, bias=neg_mean[:, last:], scale=1.0
+        )
+        nc.vector.tensor_copy(query_grouped[:], query_raw[:].rearrange("p t q -> p q t"))
         q_codes = held.tile([P, Q], U32, name="q_codes", align_bytes=64)
         q_scales = held.tile([P, Q], U8, name="q_scales", align_bytes=64)
         quantise(q_codes[:], q_scales[:], query_grouped[:].rearrange("p q t -> p (q t)"))
+        nc.vector.tensor_tensor(
+            km[:, :VECTOR_SLOTS, 2:],
+            listed[:, 2:, :VECTOR_SLOTS].rearrange("p t i -> p i t"),
+            neg_mean[:, 2:].unsqueeze(1).to_broadcast([P, VECTOR_SLOTS, 2]),
+            ALU.add,
+        )
+        nc.vector.tensor_scalar(
+            km[:, VECTOR_SLOTS:LAST_SPLIT, last], listed[:, last, VECTOR_SLOTS:LAST_SPLIT], neg_mean[:, last:], None, ALU.add
+        )
+        pieces = (slice(3 * P, I), slice(0, 2 * P), slice(2 * P, 3 * P))
         km_codes = held.tile([P, I], U32, name="km_codes", align_bytes=64)
         km_scales = held.tile([P, I], U8, name="km_scales", align_bytes=64)
+        for cols in pieces:
+            nc.vector.quantize_mx(
+                out=km_codes[:, cols].bitcast(FP8X4), scales=km_scales[:, cols],
+                in_=km[:, cols, :].rearrange("p i t -> p (i t)"),
+            )
+
         scores = psum.tile([Q, I], F32, name="scores", tag="scores")
-        for cols in halves:
-            quantise(km_codes[:, cols], km_scales[:, cols], km[:, cols, :].rearrange("p i t -> p (i t)"))
-        for cols in halves:
+        for cols in pieces:
             nc.tensor.matmul_mx(
                 out=scores[:, cols], lhsT=q_codes[:].bitcast(FP8X4), lhsT_scale=q_scales[:],
                 rhs=km_codes[:, cols].bitcast(FP8X4), rhs_scale=km_scales[:, cols], start=True, stop=True,
             )
-
         listed_vals = [held.tile([P, I], BF16, name="listed_vals%d" % b, align_bytes=64) for b in range(BLOCKS)]
         gather_on_scalar(listed_vals[0][:], val_rows[0][:], 0, I)
         neg_max = held.tile([Q, 1], F32, name="neg_max")
@@ -150,30 +157,35 @@ def tile_attend_smoothkeys_kernel(tc, query, keys, size, vals, offs, out):
         p = place("p", [Q, I], F32, on_vals[0])
         row_sum = held.tile([Q, 1], F32, name="row_sum")
         nc.scalar.activation(p[:], scores[:], ACT.Exp, bias=neg_max[:], scale=1.0, accum_out=row_sum[:])
+        size_turned = psum.tile([P, P], F32, name="size_turned", tag="early_acc")
+        nc.tensor.transpose(size_turned[:], size_rows[:], ident[:])
+        size_cols = held.tile([P, I // P], F32, name="size_cols", tag="query_raw")
+        nc.vector.tensor_copy(size_cols[:], size_turned[:, : I // P])
+        size_bank = psum.tile([P, I // P, P], F32, name="size_bank", tag="size_bank")
+        for j in range(I // P):
+            nc.tensor.transpose(size_bank[:, j, :], size_cols[:, j : j + 1].to_broadcast([P, P]), ident[:])
         inv_sum = held.tile([Q, 1], F32, name="inv_sum")
-        nc.vector.reciprocal(inv_sum[:], row_sum[:])
+        nc.gpsimd.tensor_tensor(inv_sum[:], row_sum[:], minus_one[:], ALU.pow)
+        grouped = held.tile([P, 2, P * PACK], BF16, name="grouped", align_bytes=64)
         bank0 = turn_slots(listed_vals[0][:])
-        grouped0 = held.tile([P, P * PACK], BF16, name="grouped0", align_bytes=64)
-        nc.vector.tensor_copy(as_words(grouped0[:]), by_columns(bank0[:]))
-        v_codes = held.tile([P, 2 * P], U32, name="v_codes", align_bytes=64)
-        v_scales = held.tile([P, 2 * P], U8, name="v_scales", align_bytes=64)
-        quantise(v_codes[:, :P], v_scales[:, :P], grouped0[:])
-        gather_on_scalar(listed_vals[1][:], val_rows[1][:], 0, I)
-        w = held.tile([Q, I], BF16, name="w", align_bytes=64)
+        nc.scalar.copy(as_words(grouped[:, 0, :]), by_columns(bank0[:]))
+        gather_on_vector(listed_vals[1][:], val_rows[1][:], 0, I)
+        w = place("w", [Q, I], BF16, on_vals[1])
         nc.vector.scalar_tensor_tensor(
             w[:], p[:], inv_sum[:], size_bank[:].rearrange("q j s -> q (j s)"), ALU.mult, ALU.mult
         )
-        w_bank = turn_slots(w[:])
         bank1 = turn_slots(listed_vals[1][:])
-        gather_shared(listed_vals[2][:], val_rows[2][:], VECTOR_GATHER)
-        grouped1 = place("grouped1", [P, P * PACK], BF16, on_vals[2] + KIB)
-        nc.vector.tensor_copy(as_words(grouped1[:]), by_columns(bank1[:]))
+        nc.scalar.copy(as_words(grouped[:, 1, :]), by_columns(bank1[:]))
+        w_bank = turn_slots(w[:])
+        gather_shared(listed_vals[2][:], val_rows[2][:], THIRD_VECTOR_GATHER)
+        v_codes = place("v_codes", [P, 2 * P], U32, on_vals[2] + KIB)
+        v_scales = held.tile([P, 2 * P], U8, name="v_scales", align_bytes=64)
+        quantise(v_codes[:], v_scales[:], grouped[:].rearrange("p b c -> p (b c)"))
         w_grouped = place("w_grouped", [P, Q * PACK], BF16, on_vals[2])
         nc.scalar.copy(as_words(w_grouped[:]), by_columns(w_bank[:]))
-        quantise(v_codes[:, P:], v_scales[:, P:], grouped1[:])
         bank2 = turn_slots(listed_vals[2][:])
 
-        gather_shared(listed_vals[3][:], val_rows[3][:], VECTOR_GATHER)
+        gather_shared(listed_vals[3][:], val_rows[3][:], HALF)
         w_codes = place("w_codes", [P, Q], U32, on_vals[3])
         w_scales = held.tile([P, Q], U8, name="w_scales", align_bytes=64)
         quantise(w_codes[:], w_scales[:], w_grouped[:])

@@ -22,7 +22,6 @@ PAIRS = 2
 BLOCKS = E // P
 HALF = I // 2
 STRIPE = 16
-THIRD_VECTOR_GATHER = 320
 VECTOR_SLOTS = 256
 LAST_SPLIT = 320
 KIB = 1024
@@ -83,6 +82,19 @@ def tile_attend_smoothkeys_kernel(tc, query, keys, size, vals, offs, out):
             for u in range(PAIRS):
                 nc.tensor.transpose(bank[:, u, :], words[:, u : HALF : PAIRS], ident[:])
             return bank
+
+        def turn_parted(rows):
+            words = rows.bitcast(F32)
+            bank = turn.tile([P, PAIRS, P], F32, name="turned")
+            for u in range(PAIRS):
+                nc.tensor.transpose(bank[:, u, :], words[:, u * P : (u + 1) * P], ident[:])
+            return bank
+
+        def by_parity(rows):
+            return rows.rearrange("p (j u e) -> p u j e", u=PAIRS, e=2)
+
+        def as_parted(rows):
+            return rows.rearrange("p (u j e) -> p u j e", u=PAIRS, e=2)
 
         def as_words(grouped):
             return grouped.bitcast(F32).rearrange("p (c u) -> p c u", u=PAIRS)
@@ -156,7 +168,9 @@ def tile_attend_smoothkeys_kernel(tc, query, keys, size, vals, offs, out):
         nc.vector.tensor_reduce(neg_max[:], scores[:], AXIS.X, ALU.max, negate=True)
         p = place("p", [Q, I], F32, on_vals[0])
         row_sum = held.tile([Q, 1], F32, name="row_sum")
-        nc.scalar.activation(p[:], scores[:], ACT.Exp, bias=neg_max[:], scale=1.0, accum_out=row_sum[:])
+        nc.scalar.activation(
+            as_parted(p[:]), by_parity(scores[:]), ACT.Exp, bias=neg_max[:], scale=1.0, accum_out=row_sum[:]
+        )
         size_turned = psum.tile([P, P], F32, name="size_turned", tag="early_acc")
         nc.tensor.transpose(size_turned[:], size_rows[:], ident[:])
         size_cols = held.tile([P, I // P], F32, name="size_cols", tag="query_raw")
@@ -171,18 +185,20 @@ def tile_attend_smoothkeys_kernel(tc, query, keys, size, vals, offs, out):
         nc.scalar.copy(as_words(grouped[:, 0, :]), by_columns(bank0[:]))
         gather_on_vector(listed_vals[1][:], val_rows[1][:], 0, I)
         w = place("w", [Q, I], BF16, on_vals[1])
-        nc.vector.scalar_tensor_tensor(
-            w[:], p[:], inv_sum[:], size_bank[:].rearrange("q j s -> q (j s)"), ALU.mult, ALU.mult
-        )
+        for u in range(PAIRS):
+            nc.vector.scalar_tensor_tensor(
+                as_parted(w[:])[:, u], as_parted(p[:])[:, u], inv_sum[:],
+                by_parity(size_bank[:].rearrange("q j s -> q (j s)"))[:, u], ALU.mult, ALU.mult,
+            )
         bank1 = turn_slots(listed_vals[1][:])
         nc.scalar.copy(as_words(grouped[:, 1, :]), by_columns(bank1[:]))
-        w_bank = turn_slots(w[:])
-        gather_shared(listed_vals[2][:], val_rows[2][:], THIRD_VECTOR_GATHER)
-        v_codes = place("v_codes", [P, 2 * P], U32, on_vals[2] + KIB)
+        w_bank = turn_parted(w[:])
+        gather_on_scalar(listed_vals[2][:], val_rows[2][:], 0, I)
+        v_codes = place("v_codes", [P, 2 * P], U32, on_vals[0])
         v_scales = held.tile([P, 2 * P], U8, name="v_scales", align_bytes=64)
         quantise(v_codes[:], v_scales[:], grouped[:].rearrange("p b c -> p (b c)"))
-        w_grouped = place("w_grouped", [P, Q * PACK], BF16, on_vals[2])
-        nc.scalar.copy(as_words(w_grouped[:]), by_columns(w_bank[:]))
+        w_grouped = held.tile([P, Q * PACK], BF16, name="w_grouped", align_bytes=64)
+        nc.vector.tensor_copy(as_words(w_grouped[:]), by_columns(w_bank[:]))
         bank2 = turn_slots(listed_vals[2][:])
 
         gather_shared(listed_vals[3][:], val_rows[3][:], HALF)

from contextlib import ExitStack

import concourse.mybir as mybir
from concourse.masks import make_identity

D, T, I, Q, E = 512, 2048, 512, 128, 512
FLOPS = 2 * Q * I * D + 2 * Q * I * E

F32 = mybir.dt.float32
BF16 = mybir.dt.bfloat16
U32 = mybir.dt.uint32
U16 = mybir.dt.uint16
U8 = mybir.dt.uint8
FP8X4 = mybir.dt.float8_e4m3fn_x4
ACT = mybir.ActivationFunctionType
ALU = mybir.AluOpType
AXIS = mybir.AxisListType

P = 128
PACK = 4
PAIRS = 2
BLOCKS = E // P
HALF = I // 2
STRIPE = 16
VECTOR_SLOTS = 256
LAST_SPLIT = 320
KIB = 1024


def tile_attend_smoothkeys_kernel(tc, query, keys, size, vals, offs, out):
    nc = tc.nc
    with ExitStack() as ctx:
        held = ctx.enter_context(tc.tile_pool(name="held", bufs=1))
        placed = ctx.enter_context(tc.tile_pool(name="placed", bufs=1))
        psum = ctx.enter_context(tc.psum_pool(name="psum", bufs=1))
        turn = ctx.enter_context(tc.psum_pool(name="turn", bufs=3))

        def place(name, shape, dtype, offset):
            return placed.tile(shape, dtype, name=name, offset=offset, align_bytes=64)

        offsets = held.tile([P, I // STRIPE], U16, name="offsets")
        key_planes = [held.tile([P, T], F32, name="keys%d" % t) for t in range(PACK)]
        on_vals = [b * 8 * KIB for b in range(BLOCKS)]
        val_rows = [place("vals%d" % b, [P, T], F32, on_vals[b]) for b in range(BLOCKS)]
        query_raw = held.tile([P, PACK, Q], F32, name="query_raw", tag="query_raw")
        size_rows = held.tile([P, P], F32, name="size_rows")
        nc.vector.memset(size_rows[:], 0.0)

        keys_by_plane = keys.rearrange("(p t) n -> p t n", t=PACK)
        nc.sync.dma_start(key_planes[0][:], keys_by_plane[:, 0, :])
        nc.sync.dma_start(offsets[:], offs)
        for t in range(1, PACK):
            nc.sync.dma_start(key_planes[t][:], keys_by_plane[:, t, :])
        nc.sync.dma_start(query_raw[:], query.rearrange("(p t) q -> p t q", t=PACK))
        nc.sync.dma_start(size_rows[: I // P, :], size.rearrange("o (j s) -> (o j) s", s=P))
        for b in range(BLOCKS):
            nc.sync.dma_start(val_rows[b][:], vals[b * P : (b + 1) * P, :])

        ident = held.tile([P, P], F32, name="ident")
        make_identity(nc, ident[:])
        minus_one = held.tile([Q, 1], F32, name="minus_one")
        nc.gpsimd.memset(minus_one[:], -1.0)

        def gather_on_vector(rows, window, first, stop):
            nc.vector.tensor_copy(rows[:, first:stop], window.indirect(offsets[:, first // STRIPE : stop // STRIPE]))

        def gather_on_scalar(rows, window, first, stop):
            nc.scalar.activation(
                rows[:, first:stop], window.indirect(offsets[:, first // STRIPE : stop // STRIPE]), ACT.Copy
            )

        def gather_shared(rows, window, split):
            gather_on_vector(rows, window, 0, split)
            gather_on_scalar(rows, window, split, I)

        def quantise(codes, scales, grouped):
            nc.vector.quantize_mx(out=codes.bitcast(FP8X4), scales=scales, in_=grouped)

        def turn_slots(rows):
            words = rows.bitcast(F32)
            bank = turn.tile([P, PAIRS, P], F32, name="turned")
            for u in range(PAIRS):
                nc.tensor.transpose(bank[:, u, :], words[:, u : HALF : PAIRS], ident[:])
            return bank

        def turn_parted(rows):
            words = rows.bitcast(F32)
            bank = turn.tile([P, PAIRS, P], F32, name="turned")
            for u in range(PAIRS):
                nc.tensor.transpose(bank[:, u, :], words[:, u * P : (u + 1) * P], ident[:])
            return bank

        def by_parity(rows):
            return rows.rearrange("p (j u e) -> p u j e", u=PAIRS, e=2)

        def as_parted(rows):
            return rows.rearrange("p (u j e) -> p u j e", u=PAIRS, e=2)

        def as_words(grouped):
            return grouped.bitcast(F32).rearrange("p (c u) -> p c u", u=PAIRS)

        def by_columns(bank):
            return bank.rearrange("p u c -> p c u")

        km = held.tile([P, I, PACK], BF16, name="km", align_bytes=64)
        query_grouped = held.tile([P, Q, PACK], BF16, name="query_grouped", align_bytes=64)
        listed = held.tile([P, PACK, I], F32, name="listed_keys")
        neg_mean = held.tile([P, PACK], F32, name="neg_mean")
        part_mean = held.tile([P, 1], F32, name="part_mean")
        scaled = held.tile([P, I], BF16, name="scaled_keys")
        last = PACK - 1
        for t in range(last):
            nc.vector.tensor_copy(listed[:, t, :], key_planes[t][:].indirect(offsets[:]))
            nc.vector.tensor_scalar(
                scaled[:], listed[:, t, :], -1.0 / I, None, ALU.mult, ALU.add, accum_out=neg_mean[:, t : t + 1]
            )
            split = VECTOR_SLOTS if t >= 2 else 0
            nc.scalar.activation(
                km[:, split:, t], listed[:, t, split:], ACT.Identity, bias=neg_mean[:, t : t + 1], scale=1.0
            )
        for h in range(2):
            nc.vector.tensor_copy(
                listed[:, last, h * HALF : (h + 1) * HALF],
                key_planes[last][:].indirect(offsets[:, h * HALF // 16 : (h + 1) * HALF // 16]),
            )
        scaled_last = held.tile([P, I], BF16, name="scaled_last")
        nc.scalar.activation(
            scaled_last[:, :HALF], listed[:, last, :HALF], ACT.Copy, scale=-1.0 / (I * HALF), accum_out=part_mean[:]
        )
        nc.scalar.activation(
            scaled_last[:, HALF:], listed[:, last, HALF:], ACT.Identity, bias=part_mean[:], scale=-1.0 / I,
            accum_out=neg_mean[:, last:],
        )
        nc.scalar.activation(
            km[:, LAST_SPLIT:, last], listed[:, last, LAST_SPLIT:], ACT.Identity, bias=neg_mean[:, last:], scale=1.0
        )
        nc.vector.tensor_copy(query_grouped[:], query_raw[:].rearrange("p t q -> p q t"))
        q_codes = held.tile([P, Q], U32, name="q_codes", align_bytes=64)
        q_scales = held.tile([P, Q], U8, name="q_scales", align_bytes=64)
        quantise(q_codes[:], q_scales[:], query_grouped[:].rearrange("p q t -> p (q t)"))
        nc.vector.tensor_tensor(
            km[:, :VECTOR_SLOTS, 2:],
            listed[:, 2:, :VECTOR_SLOTS].rearrange("p t i -> p i t"),
            neg_mean[:, 2:].unsqueeze(1).to_broadcast([P, VECTOR_SLOTS, 2]),
            ALU.add,
        )
        nc.vector.tensor_scalar(
            km[:, VECTOR_SLOTS:LAST_SPLIT, last], listed[:, last, VECTOR_SLOTS:LAST_SPLIT], neg_mean[:, last:], None, ALU.add
        )
        pieces = (slice(3 * P, I), slice(0, 2 * P), slice(2 * P, 3 * P))
        km_codes = held.tile([P, I], U32, name="km_codes", align_bytes=64)
        km_scales = held.tile([P, I], U8, name="km_scales", align_bytes=64)
        for cols in pieces:
            nc.vector.quantize_mx(
                out=km_codes[:, cols].bitcast(FP8X4), scales=km_scales[:, cols],
                in_=km[:, cols, :].rearrange("p i t -> p (i t)"),
            )

        scores = psum.tile([Q, I], F32, name="scores", tag="scores")
        for cols in pieces:
            nc.tensor.matmul_mx(
                out=scores[:, cols], lhsT=q_codes[:].bitcast(FP8X4), lhsT_scale=q_scales[:],
                rhs=km_codes[:, cols].bitcast(FP8X4), rhs_scale=km_scales[:, cols], start=True, stop=True,
            )
        listed_vals = [held.tile([P, I], BF16, name="listed_vals%d" % b, align_bytes=64) for b in range(BLOCKS)]
        gather_on_scalar(listed_vals[0][:], val_rows[0][:], 0, I)
        neg_max = held.tile([Q, 1], F32, name="neg_max")
        nc.vector.tensor_reduce(neg_max[:], scores[:], AXIS.X, ALU.max, negate=True)
        p = place("p", [Q, I], F32, on_vals[0])
        row_sum = held.tile([Q, 1], F32, name="row_sum")
        nc.scalar.activation(
            as_parted(p[:]), by_parity(scores[:]), ACT.Exp, bias=neg_max[:], scale=1.0, accum_out=row_sum[:]
        )
        size_turned = psum.tile([P, P], F32, name="size_turned", tag="early_acc")
        nc.tensor.transpose(size_turned[:], size_rows[:], ident[:])
        size_cols = held.tile([P, I // P], F32, name="size_cols", tag="query_raw")
        nc.vector.tensor_copy(size_cols[:], size_turned[:, : I // P])
        size_bank = psum.tile([P, I // P, P], F32, name="size_bank", tag="size_bank")
        for j in range(I // P):
            nc.tensor.transpose(size_bank[:, j, :], size_cols[:, j : j + 1].to_broadcast([P, P]), ident[:])
        inv_sum = held.tile([Q, 1], F32, name="inv_sum")
        nc.gpsimd.tensor_tensor(inv_sum[:], row_sum[:], minus_one[:], ALU.pow)
        grouped = held.tile([P, 2, P * PACK], BF16, name="grouped", align_bytes=64)
        bank0 = turn_slots(listed_vals[0][:])
        nc.scalar.copy(as_words(grouped[:, 0, :]), by_columns(bank0[:]))
        gather_on_vector(listed_vals[1][:], val_rows[1][:], 0, I)
        w = place("w", [Q, I], BF16, on_vals[1])
        for u in range(PAIRS):
            nc.vector.scalar_tensor_tensor(
                as_parted(w[:])[:, u], as_parted(p[:])[:, u], inv_sum[:],
                by_parity(size_bank[:].rearrange("q j s -> q (j s)"))[:, u], ALU.mult, ALU.mult,
            )
        bank1 = turn_slots(listed_vals[1][:])
        nc.scalar.copy(as_words(grouped[:, 1, :]), by_columns(bank1[:]))
        w_bank = turn_parted(w[:])
        gather_on_scalar(listed_vals[2][:], val_rows[2][:], 0, I)
        v_codes = place("v_codes", [P, 2 * P], U32, on_vals[0])
        v_scales = held.tile([P, 2 * P], U8, name="v_scales", align_bytes=64)
        quantise(v_codes[:], v_scales[:], grouped[:].rearrange("p b c -> p (b c)"))
        w_grouped = held.tile([P, Q * PACK], BF16, name="w_grouped", align_bytes=64)
        nc.vector.tensor_copy(as_words(w_grouped[:]), by_columns(w_bank[:]))
        bank2 = turn_slots(listed_vals[2][:])

        gather_shared(listed_vals[3][:], val_rows[3][:], HALF)
        w_codes = place("w_codes", [P, Q], U32, on_vals[3])
        w_scales = held.tile([P, Q], U8, name="w_scales", align_bytes=64)
        quantise(w_codes[:], w_scales[:], w_grouped[:])
        grouped2 = place("grouped2", [P, P * PACK], BF16, on_vals[3] + KIB)
        nc.scalar.copy(as_words(grouped2[:]), by_columns(bank2[:]))
        codes2 = held.tile([P, P], U32, name="codes2", align_bytes=64)
        scales2 = held.tile([P, P], U8, name="scales2", align_bytes=64)
        quantise(codes2[:], scales2[:], grouped2[:])

        def multiply(acc, codes, scales):
            nc.tensor.matmul_mx(
                out=acc, lhsT=w_codes[:].bitcast(FP8X4), lhsT_scale=w_scales[:],
                rhs=codes.bitcast(FP8X4), rhs_scale=scales, start=True, stop=True,
            )

        last_bank = turn_slots(listed_vals[3][:])
        early_acc = psum.tile([Q, 2 * P], F32, name="early_acc", tag="early_acc")
        multiply(early_acc[:], v_codes[:], v_scales[:])
        third_acc = psum.tile([Q, P], F32, name="third_acc")
        multiply(third_acc[:], codes2[:], scales2[:])
        width = P // 2
        last_parts = []
        for h in range(2):
            part = held.tile([P, width * PACK], BF16, name="last%d" % h, align_bytes=64)
            nc.scalar.copy(as_words(part[:]), by_columns(last_bank[:, :, h * width : (h + 1) * width]))
            codes = held.tile([P, width], U32, name="last_codes%d" % h, align_bytes=64)
            scales = held.tile([P, width], U8, name="last_scales%d" % h, align_bytes=64)
            quantise(codes[:], scales[:], part[:])
            last_parts.append((codes, scales))
        early_result = held.tile([Q, 2 * P], F32, name="early_result")
        nc.scalar.copy(early_result[:], early_acc[:])
        nc.sync.dma_start(out[:, : 2 * P], early_result[:])
        third_result = held.tile([Q, P], F32, name="third_result")
        nc.scalar.copy(third_result[:], third_acc[:])
        nc.sync.dma_start(out[:, 2 * P : 3 * P], third_result[:])
        for h, (codes, scales) in enumerate(last_parts):
            acc = psum.tile([Q, width], F32, name="last_acc%d" % h, tag=("scores", "size_bank")[h])
            multiply(acc[:], codes[:], scales[:])
            result = held.tile([Q, width], F32, name="last_result%d" % h)
            nc.vector.tensor_copy(result[:], acc[:])
            first_col = 3 * P + h * width
            nc.sync.dma_start(out[:, first_col : first_col + width], result[:])
